import numpy as np
import ml_dtypes


def mxq(x, axis, fmt="e4m3"):
    dtype, down = {"e4m3": (ml_dtypes.float8_e4m3fn, 7), "e5m2": (ml_dtypes.float8_e5m2, 14)}[fmt]
    v = np.moveaxis(np.asarray(x, np.float32).astype(ml_dtypes.bfloat16).astype(np.float64), axis, -1)
    blocks = v.reshape(v.shape[:-1] + (-1, 32))
    amax = np.abs(blocks).max(-1, keepdims=True)
    byte = np.maximum(np.where(amax > 0, np.frexp(amax)[1] - 1 + 127, 0) - down, 1)
    scale = np.exp2(byte - 127.0)
    codes = (blocks / scale).astype(np.float32).astype(dtype).astype(np.float64)
    return np.moveaxis((codes * scale).reshape(v.shape), -1, axis)


WIDE = False


def mx_kscale(k):
    if not WIDE:
        return np.ones(k)
    levels = np.array([10, -10, 5, -5, 0])
    if k % 512:
        return np.exp2(np.random.permutation(np.resize(levels, k // 32))).repeat(32)
    a = np.empty((k // 512, 16))
    for p in range(k // 512):
        a[p, :8] = np.random.permutation(np.resize(levels, 8))
        for g in range(8):
            far = levels[np.abs(levels - a[p, g]) >= 10]
            a[p, g + 8] = far[np.random.randint(len(far))]
    return np.exp2(a.ravel()).repeat(32)


def f64(x):
    return np.asarray(x).astype(np.float64)


def striped(idx):
    return np.tile(idx.reshape(-1, 16).T, (8, 1)).astype(np.uint16)


def unstriped(offs):
    return offs[:16].T.reshape(-1).astype(np.int64)


E2M1 = np.array([0.0, 0.5, 1.0, 1.5, 2.0, 3.0, 4.0, 6.0, -0.0, -0.5, -1.0, -1.5, -2.0, -3.0, -4.0, -6.0])


def pack_weight(w, fmt):
    k, n = w.shape
    w = f64(np.asarray(w, np.float32).astype(ml_dtypes.bfloat16)).reshape(k // 32, 32, n)
    amax = np.abs(w).max(1)
    if fmt == "e4m3":
        byte = np.frexp(amax)[1] - 1 + 127 - 7
    else:
        mant, ex = np.frexp(amax / 6.0)
        byte = np.where(mant > 0.5, ex, ex - 1) + 127
    byte = np.clip(np.where(amax > 0, byte, 1), 1, 254)
    scaled = (w * np.exp2(127.0 - byte)[:, None, :]).reshape(k, n).astype(np.float32)
    by_word = np.ascontiguousarray(scaled.reshape(k // 512, 128, 4, n).transpose(0, 1, 3, 2))
    if fmt == "e4m3":
        words = by_word.astype(ml_dtypes.float8_e4m3fn).view(np.uint8)
    else:
        c = by_word.astype(ml_dtypes.float4_e2m1fn).view(np.uint8) & 0xF
        words = (c[..., 0::2] | (c[..., 1::2] << 4)).reshape(k // 512, 128, 2 * n)
    return np.ascontiguousarray(words), np.ascontiguousarray(byte.astype(np.uint8).reshape(k // 512, 16, n))


def unpack_weight(words, scales, fmt):
    g, _, n = scales.shape
    words = np.ascontiguousarray(words).reshape(g, 128, n, -1)
    if fmt == "e4m3":
        vals = words.view(ml_dtypes.float8_e4m3fn).astype(np.float64)
    else:
        nib = np.empty((g, 128, n, 4), np.uint8)
        nib[..., 0::2] = words & 0xF
        nib[..., 1::2] = words >> 4
        vals = E2M1[nib]
    vals = vals * np.repeat(np.exp2(scales.astype(np.float64) - 127.0), 8, axis=1)[..., None]
    return vals.transpose(0, 1, 3, 2).reshape(g * 512, n)


def gelu(v):
    return 0.5 * v * (1.0 + np.tanh(np.sqrt(2.0 / np.pi) * (v + 0.044715 * v**3)))


K, T, S, H, N = 1024, 2048, 1024, 512, 256

def setup_inputs():
    n = np.random.standard_normal
    s = mx_kscale(K)[:, None]
    u = mx_kscale(H)[:, None]
    tab_words, tab_scales = pack_weight(n((K, T)) * s, "e4m3")
    wb_words, wb_scales = pack_weight(n((K, H)) / np.sqrt(K) / s * u.T, "e4m3")
    wc_words, wc_scales = pack_weight(n((K, H)) / np.sqrt(K) / s * u.T, "e2m1")
    return {
        "tab_words": tab_words, "tab_scales": tab_scales,
        "offs": striped(np.random.permutation(T)[:S]),
        "wa": (n((K, H)) / np.sqrt(K) / s * u.T).astype(np.float32),
        "wb_words": wb_words, "wb_scales": wb_scales,
        "wc_words": wc_words, "wc_scales": wc_scales,
        "gT": np.exp(-0.5 * np.abs(n((H, T)))).astype(np.float32),
        "w2": (n((H, N)) / np.sqrt(H) / u).astype(np.float32),
        "b2": (0.5 * n(N)).astype(np.float32),
    }

def reference(tab_words, tab_scales, offs, wa, wb_words, wb_scales, wc_words, wc_scales, gT, w2, b2):
    v = unpack_weight(tab_words, tab_scales, "e4m3")[:, unstriped(offs)]
    g = f64(gT)[:, unstriped(offs)]
    qa = mxq(f64(wa), 0, "e4m3")
    qb = unpack_weight(wb_words, wb_scales, "e4m3")
    qc = unpack_weight(wc_words, wc_scales, "e2m1")
    a = qa.T @ v
    b = qb.T @ v
    c = qc.T @ v
    h = np.maximum(np.maximum(a, b), c) * g
    y = mxq(f64(w2), 0, "e4m3").T @ mxq(h, 0, "e4m3")
    return y + f64(b2)[:, None]

@@ -1,0 +1,268 @@
+from contextlib import ExitStack
+
+import concourse.mybir as mybir
+
+K, T, S, H, N = 1024, 2048, 1024, 512, 256
+FLOPS = 2 * K * H * S * 3 + 2 * H * N * S
+
+F32 = mybir.dt.float32
+BF16 = mybir.dt.bfloat16
+I32 = mybir.dt.int32
+U32 = mybir.dt.uint32
+U16 = mybir.dt.uint16
+U8 = mybir.dt.uint8
+E4M3 = mybir.dt.float8_e4m3fn_x4
+E2M1 = mybir.dt.float4_e2m1fn_x4
+MAX = mybir.AluOpType.max
+MULT = mybir.AluOpType.mult
+ADD = mybir.AluOpType.add
+IDENTITY = mybir.ActivationFunctionType.Identity
+
+P = 128
+PACK = 4
+PASSES = K // (P * PACK)
+HALF = 512
+CHUNKS = ((0, 512), (512, 256), (768, 128), (896, 128))
+
+
+def tile_list_fresh_passage_banks_kernel(
+    tc, tab_words, tab_scales, offs, wa, wb_words, wb_scales, wc_words, wc_scales, gT, w2, b2, out
+):
+    nc = tc.nc
+    with ExitStack() as ctx:
+        keep = ctx.enter_context(tc.tile_pool(name="keep", bufs=1))
+        lane = ctx.enter_context(tc.tile_pool(name="lane", bufs=1))
+        psum = ctx.enter_context(tc.psum_pool(name="psum", bufs=1))
+
+        def sb(name, shape, dtype, tag=""):
+            return keep.tile(shape, dtype, name=name, tag=tag or name, align_bytes=64)
+
+        def bank(i):
+            return psum.tile([P, HALF], F32, name="bank%d" % i)
+
+        offsets = keep.tile([P, S // 16], U16, name="offsets")
+        nc.sync.dma_start(offsets[:], offs)
+
+        def picks(j0, width):
+            return offsets[:, j0 // 16 : (j0 + width) // 16]
+
+        warm_in = sb("warm_in", [P, 1], F32, "big0")
+        warm_out = lane.tile([P, 1], F32, name="warm_out", align_bytes=64, offset=1536)
+        nc.gpsimd.memset(warm_in[:], 0.0)
+        nc.scalar.activation(warm_out[:], warm_in[:], IDENTITY)
+        tab_plane = sb("tab_plane", [P, T], U8, "big3")
+        nc.vector.memset(tab_plane[:].bitcast(I32), 0)
+        w_plane_raw = lane.tile([P, PASSES * H], U8, name="w_plane_raw", align_bytes=64, offset=1536)
+        nc.vector.memset(w_plane_raw[:].bitcast(I32), 0)
+        v_plane1 = sb("v_plane1", [P, S], U8)
+        nc.gpsimd.memset(v_plane1[:].bitcast(I32), 0)
+
+        wc_raw = sb("wc_raw", [P, PASSES, H // 2], I32, "big1")
+        nc.sync.dma_start(wc_raw[:], wc_words.rearrange("a p e -> p a e").bitcast(I32))
+        wb_raw = sb("wb_raw", [P, PASSES, H], I32, "big2")
+        nc.sync.dma_start(wb_raw[:], wb_words.rearrange("a p e i -> p a (e i)").bitcast(I32))
+        for q in range(4):
+            nc.sync.dma_start(
+                tab_plane[32 * q : 32 * q + 8, :].bitcast(I32),
+                tab_scales[:, 4 * q : 4 * q + 4, :].bitcast(I32),
+            )
+        tab_w, wa_raw, fresh = {}, {}, {}
+
+        def load_tab(a, tag):
+            tab_w[a] = sb("tab_w%d" % a, [P, T], I32, tag)
+            nc.sync.dma_start(tab_w[a][:], tab_words[a].rearrange("p t i -> p (t i)").bitcast(I32))
+
+        def load_wa(a, tag):
+            wa_raw[a] = sb("wa_raw%d" % a, [P, PACK, H], F32, tag)
+            nc.sync.dma_start(wa_raw[a][:], wa[512 * a : 512 * (a + 1), :].rearrange("(p i) e -> p i e", i=PACK))
+
+        def load_fresh(t, tag):
+            fresh[t] = sb("fresh%d" % t, [P, T], F32, tag)
+            nc.sync.dma_start(fresh[t][:], gT.rearrange("(p t) c -> t p c", t=PACK)[t])
+
+        load_tab(0, "big0")
+        for row, scales in ((0, wc_scales), (4, wb_scales)):
+            for q in range(4):
+                nc.scalar.dma_start(
+                    w_plane_raw[32 * q + row : 32 * q + row + 4, :].bitcast(I32),
+                    scales[:, 4 * q : 4 * q + 4, :].rearrange("a r e -> r a e").bitcast(I32),
+                )
+
+        wc_codes = sb("wc_codes", [P, PASSES, H], U16)
+        nc.vector.tensor_copy(
+            wc_codes[:].rearrange("p a (t m) -> p a m t", t=PACK),
+            wc_raw[:].bitcast(U16).rearrange("p a (m t) -> p a m t", t=PACK),
+        )
+        wb_codes = sb("wb_codes", [P, PASSES, H], I32)
+        nc.vector.tensor_copy(
+            wb_codes[:].rearrange("p a (t m) -> p a m t", t=PACK),
+            wb_raw[:].rearrange("p a (m t) -> p a m t", t=PACK),
+        )
+        load_wa(0, "big1")
+        load_tab(1, "big2")
+        v_plane = sb("v_plane", [P, S], U8)
+        nc.vector.tensor_copy(v_plane[:], tab_plane[:].indirect(offsets[:]))
+        for q in range(4):
+            nc.scalar.dma_start(
+                v_plane1[32 * q : 32 * q + 4, :].bitcast(I32), v_plane[32 * q + 4 : 32 * q + 8, :].bitcast(I32)
+            )
+        load_wa(1, "big3")
+        w_plane = sb("w_plane", [P, PASSES, H], U8)
+        nc.vector.tensor_copy(
+            w_plane[:].rearrange("p a (t m) -> p a m t", t=PACK),
+            w_plane_raw[:].rearrange("p (a m t) -> p a m t", a=PASSES, t=PACK),
+        )
+
+        v_codes = {}
+
+        def gather_codes(a, hf, tag=""):
+            if (a, hf) == (1, 0):
+                v_codes[a, hf] = lane.tile([P, HALF], U32, name="v_codes1_0", align_bytes=64, offset=0)
+            else:
+                v_codes[a, hf] = sb("v_codes%d_%d" % (a, hf), [P, HALF], U32, tag)
+            nc.vector.tensor_copy(v_codes[a, hf][:], tab_w[a][:].bitcast(U32).indirect(picks(hf * HALF, HALF)))
+
+        gather_codes(0, 0)
+        gather_codes(0, 1)
+        gather_codes(1, 0)
+
+        def first_product(acc, codes, scales, a, hf, moving_scales):
+            nc.tensor.matmul_mx(
+                out=acc[:], lhsT=codes, lhsT_scale=scales,
+                rhs=v_codes[a, hf][:].bitcast(E4M3), rhs_scale=moving_scales,
+                start=(a == 0), stop=(a == PASSES - 1),
+            )
+
+        def v_scales(a, hf):
+            return v_plane[4 * a : P, hf * HALF : (hf + 1) * HALF]
+
+        def b_pass(acc, t, a, hf):
+            cols = slice(t * P, (t + 1) * P)
+            first_product(acc, wb_codes[:, a, cols].bitcast(E4M3), w_plane[4:P, a, cols], a, hf, v_scales(a, hf))
+
+        def c_pass(acc, t, a, hf):
+            cols = slice(t * P, (t + 1) * P)
+            moving = v_scales(0, hf) if a == 0 else v_plane1[:, hf * HALF : (hf + 1) * HALF]
+            first_product(acc, wc_codes[:, a, cols].bitcast(E2M1), w_plane[:, a, cols], a, hf, moving)
+
+        best_bc = {}
+
+        def max_bc(acc_b, acc_c, t, hf):
+            b_sb = sb("b_sb%d_%d" % (t, hf), [P, HALF], F32)
+            nc.scalar.copy(b_sb[:], acc_b[:])
+            best_bc[t, hf] = sb("best_bc%d_%d" % (t, hf), [P, HALF], F32, "best3_0" if (t, hf) == (3, 1) else "")
+            nc.vector.tensor_tensor(best_bc[t, hf][:], acc_c[:], b_sb[:], MAX)
+
+        wa_bf, wa_codes, wa_plane = {}, {}, {}
+
+        def round_wa(a, copy):
+            wa_bf[a] = sb("wa_bf%d" % a, [P, H * PACK], BF16)
+            copy(
+                wa_bf[a][:].rearrange("p (t m i) -> p m i t", t=PACK, i=PACK),
+                wa_raw[a][:].rearrange("p i (m t) -> p m i t", t=PACK),
+            )
+
+        def quantise_wa(a):
+            wa_codes[a] = sb("wa_codes%d" % a, [P, H], U32)
+            wa_plane[a] = lane.tile([P, H], U8, name="wa_plane%d" % a, align_bytes=64, offset=2048 + H * a)
+            nc.vector.quantize_mx(out=wa_codes[a][:].bitcast(E4M3), scales=wa_plane[a][:], in_=wa_bf[a][:])
+
+        load_fresh(0, "big0")
+        round_wa(0, nc.scalar.copy)
+        load_fresh(1, "big1")
+        round_wa(1, nc.vector.tensor_copy)
+        load_fresh(3, "big3")
+        quantise_wa(0)
+        quantise_wa(1)
+        w2_raw = sb("w2_raw", [P, PACK, N], F32, "wa_bf0")
+        nc.sync.dma_start(w2_raw[:], w2.rearrange("(p t) n -> p t n", t=PACK))
+
+        bias = sb("bias", [P, N // P], F32, "wa_bf1")
+        with nc.allow_non_contiguous_dma("one bias value for each partition"):
+            nc.sync.dma_start(bias[:], b2.rearrange("(u p) -> p u", p=P))
+
+        accs = [(bank(t), bank(4 + t)) for t in range(PACK)]
+        for t in range(PACK):
+            b_pass(accs[t][0], t, 0, 0)
+            c_pass(accs[t][1], t, 0, 0)
+        for t in range(PACK):
+            b_pass(accs[t][0], t, 1, 0)
+            c_pass(accs[t][1], t, 1, 0)
+            max_bc(accs[t][0], accs[t][1], t, 0)
+            if t == 0:
+                gather_codes(1, 1, "b_sb0_0")
+                load_fresh(2, "big2")
+
+        best = {}
+
+        def max_abc(t, hf):
+            acc = bank(4 * (1 - hf) + t)
+            cols = slice(t * P, (t + 1) * P)
+            for a in range(PASSES):
+                first_product(acc, wa_codes[a][:, cols].bitcast(E4M3), wa_plane[a][:, cols], a, hf, v_scales(a, hf))
+            best[t, hf] = sb("best%d_%d" % (t, hf), [P, HALF], F32)
+            nc.vector.tensor_tensor(best[t, hf][:], acc[:], best_bc[t, hf][:], MAX)
+
+        h_f32, h_bf = {}, {}
+
+        def weigh(c, t):
+            j0, width = CHUNKS[c]
+            if t == 0:
+                h_f32[c] = sb("h_f32_%d" % c, [P, PACK, width], F32, ("", "best3_0", "h_bf0", "h_bf1")[c])
+            nc.vector.tensor_tensor(
+                h_f32[c][:, t, :], fresh[t][:].indirect(picks(j0, width)),
+                best[t, j0 // HALF][:, j0 % HALF : j0 % HALF + width], MULT,
+            )
+
+        def round_h(c):
+            width = CHUNKS[c][1]
+            h_bf[c] = sb("h_bf%d" % c, [P, width * PACK], BF16)
+            nc.scalar.copy(
+                h_bf[c][:].rearrange("p (c i t) -> p c t i", t=PACK, i=4),
+                h_f32[c][:].rearrange("p t (c i) -> p c t i", i=4),
+            )
+
+        def mix(c):
+            j0, width = CHUNKS[c]
+            h_codes = sb("h_codes%d" % c, [P, width], U32)
+            h_plane = sb("h_plane%d" % c, [P, width], U8)
+            nc.vector.quantize_mx(out=h_codes[:].bitcast(E4M3), scales=h_plane[:], in_=h_bf[c][:])
+            res = sb("res%d" % c, [P, N // P, width], F32)
+            for u in range(N // P):
+                acc = bank(4 + (2 * c + u) % 4)
+                cols = slice(u * P, (u + 1) * P)
+                nc.tensor.matmul_mx(
+                    out=acc[:, 0:width], lhsT=w2_codes[:, cols].bitcast(E4M3), lhsT_scale=w2_plane[:, cols],
+                    rhs=h_codes[:].bitcast(E4M3), rhs_scale=h_plane[:], start=True, stop=True,
+                )
+                nc.scalar.activation(res[:, u, :], acc[:, 0:width], IDENTITY, bias=bias[:, u : u + 1])
+            nc.sync.dma_start(out.rearrange("(u p) j -> p u j", p=P)[:, :, j0 : j0 + width], res[:])
+
+        for t in range(PACK):
+            max_abc(t, 0)
+            weigh(0, t)
+        round_h(0)
+        w2_bf = sb("w2_bf", [P, N * PACK], BF16)
+        nc.scalar.copy(
+            w2_bf[:].rearrange("p (c i t) -> p c t i", t=PACK, i=4),
+            w2_raw[:].rearrange("p t (c i) -> p c t i", i=4),
+        )
+        w2_codes = sb("w2_codes", [P, N], U32)
+        w2_plane = sb("w2_plane", [P, N], U8)
+        for t in range(PACK):
+            acc_b, acc_c = bank(t), bank(4 + t)
+            for a in range(PASSES):
+                b_pass(acc_b, t, a, 1)
+            for a in range(PASSES):
+                c_pass(acc_c, t, a, 1)
+            max_bc(acc_b, acc_c, t, 1)
+            max_abc(t, 1)
+        nc.vector.quantize_mx(out=w2_codes[:].bitcast(E4M3), scales=w2_plane[:], in_=w2_bf[:])
+        mix(0)
+        for c in range(1, len(CHUNKS)):
+            for t in range(PACK):
+                weigh(c, t)
+            round_h(c)
+            if c > 1:
+                mix(c - 1)
+        mix(len(CHUNKS) - 1)

@@ -15,14 +15,14 @@ E4M3 = mybir.dt.float8_e4m3fn_x4
 E2M1 = mybir.dt.float4_e2m1fn_x4
 MAX = mybir.AluOpType.max
 MULT = mybir.AluOpType.mult
-ADD = mybir.AluOpType.add
 IDENTITY = mybir.ActivationFunctionType.Identity
 
 P = 128
 PACK = 4
 PASSES = K // (P * PACK)
 HALF = 512
-CHUNKS = ((0, 512), (512, 256), (768, 128), (896, 128))
+QUARTER = 256
+UNITS = PACK * S // HALF
 
 
 def tile_list_fresh_passage_banks_kernel(
@@ -31,7 +31,6 @@ def tile_list_fresh_passage_banks_kernel(
     nc = tc.nc
     with ExitStack() as ctx:
         keep = ctx.enter_context(tc.tile_pool(name="keep", bufs=1))
-        lane = ctx.enter_context(tc.tile_pool(name="lane", bufs=1))
         psum = ctx.enter_context(tc.psum_pool(name="psum", bufs=1))
 
         def sb(name, shape, dtype, tag=""):
@@ -46,26 +45,6 @@ def tile_list_fresh_passage_banks_kernel(
         def picks(j0, width):
             return offsets[:, j0 // 16 : (j0 + width) // 16]
 
-        warm_in = sb("warm_in", [P, 1], F32, "big0")
-        warm_out = lane.tile([P, 1], F32, name="warm_out", align_bytes=64, offset=1536)
-        nc.gpsimd.memset(warm_in[:], 0.0)
-        nc.scalar.activation(warm_out[:], warm_in[:], IDENTITY)
-        tab_plane = sb("tab_plane", [P, T], U8, "big3")
-        nc.vector.memset(tab_plane[:].bitcast(I32), 0)
-        w_plane_raw = lane.tile([P, PASSES * H], U8, name="w_plane_raw", align_bytes=64, offset=1536)
-        nc.vector.memset(w_plane_raw[:].bitcast(I32), 0)
-        v_plane1 = sb("v_plane1", [P, S], U8)
-        nc.gpsimd.memset(v_plane1[:].bitcast(I32), 0)
-
-        wc_raw = sb("wc_raw", [P, PASSES, H // 2], I32, "big1")
-        nc.sync.dma_start(wc_raw[:], wc_words.rearrange("a p e -> p a e").bitcast(I32))
-        wb_raw = sb("wb_raw", [P, PASSES, H], I32, "big2")
-        nc.sync.dma_start(wb_raw[:], wb_words.rearrange("a p e i -> p a (e i)").bitcast(I32))
-        for q in range(4):
-            nc.sync.dma_start(
-                tab_plane[32 * q : 32 * q + 8, :].bitcast(I32),
-                tab_scales[:, 4 * q : 4 * q + 4, :].bitcast(I32),
-            )
         tab_w, wa_raw, fresh = {}, {}, {}
 
         def load_tab(a, tag):
@@ -80,189 +59,207 @@ def tile_list_fresh_passage_banks_kernel(
             fresh[t] = sb("fresh%d" % t, [P, T], F32, tag)
             nc.sync.dma_start(fresh[t][:], gT.rearrange("(p t) c -> t p c", t=PACK)[t])
 
-        load_tab(0, "big0")
-        for row, scales in ((0, wc_scales), (4, wb_scales)):
+        def load_scales(queue, plane, row, scales):
             for q in range(4):
-                nc.scalar.dma_start(
-                    w_plane_raw[32 * q + row : 32 * q + row + 4, :].bitcast(I32),
+                queue.dma_start(
+                    plane[32 * q + row : 32 * q + row + 4, :].bitcast(I32),
                     scales[:, 4 * q : 4 * q + 4, :].rearrange("a r e -> r a e").bitcast(I32),
                 )
 
-        wc_codes = sb("wc_codes", [P, PASSES, H], U16)
-        nc.vector.tensor_copy(
-            wc_codes[:].rearrange("p a (t m) -> p a m t", t=PACK),
-            wc_raw[:].bitcast(U16).rearrange("p a (m t) -> p a m t", t=PACK),
-        )
+        tab_plane = sb("tab_plane", [P, PASSES * T], U8, "stage3")
+        nc.vector.memset(tab_plane[:].bitcast(I32), 0)
+        warm_in = sb("warm_in", [P, 1], F32, "stage5")
+        warm_out = sb("warm_out", [P, 1], F32, "stage4")
+        nc.vector.memset(warm_in[:], 0.0)
+        nc.scalar.activation(warm_out[:], warm_in[:], IDENTITY)
+
+        load_tab(0, "stage0")
+        wb_raw = sb("wb_raw", [P, PASSES, H], I32, "stage1")
+        nc.sync.dma_start(wb_raw[:], wb_words.rearrange("a p e i -> p a (e i)").bitcast(I32))
+        wc_raw = sb("wc_raw", [P, PASSES, H // 2], I32, "stage2")
+        nc.sync.dma_start(wc_raw[:], wc_words.rearrange("a p e -> p a e").bitcast(I32))
+        load_scales(nc.sync, tab_plane, 0, tab_scales)
+        load_wa(0, "stage4")
+        w_plane_raw = sb("w_plane_raw", [P, PASSES * H], U8, "stage5")
+        nc.gpsimd.memset(w_plane_raw[:].bitcast(I32), 0)
+        load_scales(nc.scalar, w_plane_raw, 4, wb_scales)
+        load_scales(nc.scalar, w_plane_raw, 0, wc_scales)
+
+        v_codes, v_plane = {}, {}
+
+        def gather_codes(a, hf):
+            v_codes[a, hf] = sb("v_codes%d_%d" % (a, hf), [P, HALF], U32)
+            nc.vector.tensor_copy(v_codes[a, hf][:], tab_w[a][:].bitcast(U32).indirect(picks(hf * HALF, HALF)))
+
+        gather_codes(0, 0)
+        gather_codes(0, 1)
+        load_wa(1, "stage0")
         wb_codes = sb("wb_codes", [P, PASSES, H], I32)
         nc.vector.tensor_copy(
             wb_codes[:].rearrange("p a (t m) -> p a m t", t=PACK),
             wb_raw[:].rearrange("p a (m t) -> p a m t", t=PACK),
         )
-        load_wa(0, "big1")
-        load_tab(1, "big2")
-        v_plane = sb("v_plane", [P, S], U8)
-        nc.vector.tensor_copy(v_plane[:], tab_plane[:].indirect(offsets[:]))
-        for q in range(4):
-            nc.scalar.dma_start(
-                v_plane1[32 * q : 32 * q + 4, :].bitcast(I32), v_plane[32 * q + 4 : 32 * q + 8, :].bitcast(I32)
-            )
-        load_wa(1, "big3")
+        load_tab(1, "stage1")
+        wc_codes = sb("wc_codes", [P, PASSES, H], U16)
+        nc.vector.tensor_copy(
+            wc_codes[:].rearrange("p a (t m) -> p a m t", t=PACK),
+            wc_raw[:].bitcast(U16).rearrange("p a (m t) -> p a m t", t=PACK),
+        )
+        load_fresh(0, "stage2")
+        for a in range(PASSES):
+            v_plane[a] = sb("v_plane%d" % a, [P, S], U8)
+            nc.vector.tensor_copy(v_plane[a][:], tab_plane[:, a * T : (a + 1) * T].indirect(offsets[:]))
         w_plane = sb("w_plane", [P, PASSES, H], U8)
         nc.vector.tensor_copy(
             w_plane[:].rearrange("p a (t m) -> p a m t", t=PACK),
             w_plane_raw[:].rearrange("p (a m t) -> p a m t", a=PASSES, t=PACK),
         )
-
-        v_codes = {}
-
-        def gather_codes(a, hf, tag=""):
-            if (a, hf) == (1, 0):
-                v_codes[a, hf] = lane.tile([P, HALF], U32, name="v_codes1_0", align_bytes=64, offset=0)
-            else:
-                v_codes[a, hf] = sb("v_codes%d_%d" % (a, hf), [P, HALF], U32, tag)
-            nc.vector.tensor_copy(v_codes[a, hf][:], tab_w[a][:].bitcast(U32).indirect(picks(hf * HALF, HALF)))
-
-        gather_codes(0, 0)
-        gather_codes(0, 1)
-        gather_codes(1, 0)
-
-        def first_product(acc, codes, scales, a, hf, moving_scales):
-            nc.tensor.matmul_mx(
-                out=acc[:], lhsT=codes, lhsT_scale=scales,
-                rhs=v_codes[a, hf][:].bitcast(E4M3), rhs_scale=moving_scales,
-                start=(a == 0), stop=(a == PASSES - 1),
-            )
-
-        def v_scales(a, hf):
-            return v_plane[4 * a : P, hf * HALF : (hf + 1) * HALF]
-
-        def b_pass(acc, t, a, hf):
-            cols = slice(t * P, (t + 1) * P)
-            first_product(acc, wb_codes[:, a, cols].bitcast(E4M3), w_plane[4:P, a, cols], a, hf, v_scales(a, hf))
-
-        def c_pass(acc, t, a, hf):
-            cols = slice(t * P, (t + 1) * P)
-            moving = v_scales(0, hf) if a == 0 else v_plane1[:, hf * HALF : (hf + 1) * HALF]
-            first_product(acc, wc_codes[:, a, cols].bitcast(E2M1), w_plane[:, a, cols], a, hf, moving)
-
-        best_bc = {}
-
-        def max_bc(acc_b, acc_c, t, hf):
-            b_sb = sb("b_sb%d_%d" % (t, hf), [P, HALF], F32)
-            nc.scalar.copy(b_sb[:], acc_b[:])
-            best_bc[t, hf] = sb("best_bc%d_%d" % (t, hf), [P, HALF], F32, "best3_0" if (t, hf) == (3, 1) else "")
-            nc.vector.tensor_tensor(best_bc[t, hf][:], acc_c[:], b_sb[:], MAX)
+        load_fresh(1, "stage5")
 
         wa_bf, wa_codes, wa_plane = {}, {}, {}
 
-        def round_wa(a, copy):
+        def round_wa(a):
             wa_bf[a] = sb("wa_bf%d" % a, [P, H * PACK], BF16)
-            copy(
+            nc.scalar.copy(
                 wa_bf[a][:].rearrange("p (t m i) -> p m i t", t=PACK, i=PACK),
                 wa_raw[a][:].rearrange("p i (m t) -> p m i t", t=PACK),
             )
 
         def quantise_wa(a):
             wa_codes[a] = sb("wa_codes%d" % a, [P, H], U32)
-            wa_plane[a] = lane.tile([P, H], U8, name="wa_plane%d" % a, align_bytes=64, offset=2048 + H * a)
+            wa_plane[a] = sb("wa_plane%d" % a, [P, H], U8)
             nc.vector.quantize_mx(out=wa_codes[a][:].bitcast(E4M3), scales=wa_plane[a][:], in_=wa_bf[a][:])
 
-        load_fresh(0, "big0")
-        round_wa(0, nc.scalar.copy)
-        load_fresh(1, "big1")
-        round_wa(1, nc.vector.tensor_copy)
-        load_fresh(3, "big3")
-        quantise_wa(0)
-        quantise_wa(1)
-        w2_raw = sb("w2_raw", [P, PACK, N], F32, "wa_bf0")
+        round_wa(0)
+        w2_raw = sb("w2_raw", [P, PACK, N], F32, "stage4")
         nc.sync.dma_start(w2_raw[:], w2.rearrange("(p t) n -> p t n", t=PACK))
-
-        bias = sb("bias", [P, N // P], F32, "wa_bf1")
+        round_wa(1)
+        load_fresh(2, "stage0")
+        quantise_wa(0)
+        gather_codes(1, 0)
+        quantise_wa(1)
+        gather_codes(1, 1)
+        load_fresh(3, "stage1")
+        bias = sb("bias", [P, N // P], F32, "stage3")
         with nc.allow_non_contiguous_dma("one bias value for each partition"):
             nc.sync.dma_start(bias[:], b2.rearrange("(u p) -> p u", p=P))
 
-        accs = [(bank(t), bank(4 + t)) for t in range(PACK)]
-        for t in range(PACK):
-            b_pass(accs[t][0], t, 0, 0)
-            c_pass(accs[t][1], t, 0, 0)
-        for t in range(PACK):
-            b_pass(accs[t][0], t, 1, 0)
-            c_pass(accs[t][1], t, 1, 0)
-            max_bc(accs[t][0], accs[t][1], t, 0)
-            if t == 0:
-                gather_codes(1, 1, "b_sb0_0")
-                load_fresh(2, "big2")
-
-        best = {}
-
-        def max_abc(t, hf):
-            acc = bank(4 * (1 - hf) + t)
+        def stationary(kind, a, t):
             cols = slice(t * P, (t + 1) * P)
-            for a in range(PASSES):
-                first_product(acc, wa_codes[a][:, cols].bitcast(E4M3), wa_plane[a][:, cols], a, hf, v_scales(a, hf))
-            best[t, hf] = sb("best%d_%d" % (t, hf), [P, HALF], F32)
-            nc.vector.tensor_tensor(best[t, hf][:], acc[:], best_bc[t, hf][:], MAX)
+            if kind == "a":
+                return wa_codes[a][:, cols].bitcast(E4M3), wa_plane[a][:, cols]
+            if kind == "b":
+                return wb_codes[:, a, cols].bitcast(E4M3), w_plane[4:P, a, cols]
+            return wc_codes[:, a, cols].bitcast(E2M1), w_plane[:, a, cols]
 
-        h_f32, h_bf = {}, {}
+        acc = {}
 
-        def weigh(c, t):
-            j0, width = CHUNKS[c]
-            if t == 0:
-                h_f32[c] = sb("h_f32_%d" % c, [P, PACK, width], F32, ("", "best3_0", "h_bf0", "h_bf1")[c])
+        def first_pass(kind, s, a):
+            hf, t = divmod(s, PACK)
+            if a == 0:
+                acc[kind, s] = bank(2 * "abc".index(kind) + s % 2)
+            codes, scales = stationary(kind, a, t)
+            nc.tensor.matmul_mx(
+                out=acc[kind, s][:], lhsT=codes, lhsT_scale=scales,
+                rhs=v_codes[a, hf][:].bitcast(E4M3), rhs_scale=v_plane[a][:, hf * HALF : (hf + 1) * HALF],
+                start=(a == 0), stop=(a == PASSES - 1),
+            )
+
+        def first_product(kind, s):
+            for a in range(1 if s < 2 else 0, PASSES):
+                first_pass(kind, s, a)
+
+        h_first = sb("h_first", [P, PACK, HALF], F32)
+        h_last = sb("h_last", [P, 2, PACK, QUARTER], F32)
+        h_last_flat = h_last[:].rearrange("p q t c -> p (q t c)")
+
+        def a_stage(s):
+            if 2 <= s < 2 + PACK:
+                return h_first[:, s - 2, :]
+            c0 = (s - 2 - PACK) % PACK * HALF
+            return h_last_flat[:, c0 : c0 + HALF]
+
+        best_ab, best = {}, {}
+
+        def max_ab(s):
+            a_sb = a_stage(s)
+            first_product("a", s)
+            nc.scalar.copy(a_sb, acc["a", s][:])
+            first_product("b", s)
+            best_ab[s] = sb("best_ab%d" % s, [P, HALF], F32)
+            nc.vector.tensor_tensor(best_ab[s][:], acc["b", s][:], a_sb, MAX)
+
+        def max_abc(s):
+            first_product("c", s)
+            best[s] = sb("best%d" % s, [P, HALF], F32)
+            nc.vector.tensor_tensor(best[s][:], acc["c", s][:], best_ab[s][:], MAX)
+
+        def weigh(s, c0, width):
+            hf, t = divmod(s, PACK)
             nc.vector.tensor_tensor(
-                h_f32[c][:, t, :], fresh[t][:].indirect(picks(j0, width)),
-                best[t, j0 // HALF][:, j0 % HALF : j0 % HALF + width], MULT,
+                h_last[:, c0 // QUARTER, t, :] if hf else h_first[:, t, :], fresh[t][:].indirect(picks(hf * HALF + c0, width)),
+                best[s][:, c0 : c0 + width], MULT,
             )
 
-        def round_h(c):
-            width = CHUNKS[c][1]
-            h_bf[c] = sb("h_bf%d" % c, [P, width * PACK], BF16)
-            nc.scalar.copy(
-                h_bf[c][:].rearrange("p (c i t) -> p c t i", t=PACK, i=4),
-                h_f32[c][:].rearrange("p t (c i) -> p c t i", i=4),
+        def interleave(copy, dst, src):
+            copy(
+                dst.rearrange("p (c i t) -> p c t i", t=PACK, i=4),
+                src.rearrange("p t (c i) -> p c t i", i=4),
             )
 
-        def mix(c):
-            j0, width = CHUNKS[c]
-            h_codes = sb("h_codes%d" % c, [P, width], U32)
-            h_plane = sb("h_plane%d" % c, [P, width], U8)
-            nc.vector.quantize_mx(out=h_codes[:].bitcast(E4M3), scales=h_plane[:], in_=h_bf[c][:])
-            res = sb("res%d" % c, [P, N // P, width], F32)
+        def mix(j0, width, h_bf, bank0, last):
+            h_codes = sb("h_codes%d" % j0, [P, width], U32)
+            h_plane = sb("h_plane%d" % j0, [P, width], U8)
+            nc.vector.quantize_mx(out=h_codes[:].bitcast(E4M3), scales=h_plane[:], in_=h_bf[:])
             for u in range(N // P):
-                acc = bank(4 + (2 * c + u) % 4)
+                y = bank(bank0 + u)
                 cols = slice(u * P, (u + 1) * P)
                 nc.tensor.matmul_mx(
-                    out=acc[:, 0:width], lhsT=w2_codes[:, cols].bitcast(E4M3), lhsT_scale=w2_plane[:, cols],
+                    out=y[:, 0:width], lhsT=w2_codes[:, cols].bitcast(E4M3), lhsT_scale=w2_plane[:, cols],
                     rhs=h_codes[:].bitcast(E4M3), rhs_scale=h_plane[:], start=True, stop=True,
                 )
-                nc.scalar.activation(res[:, u, :], acc[:, 0:width], IDENTITY, bias=bias[:, u : u + 1])
-            nc.sync.dma_start(out.rearrange("(u p) j -> p u j", p=P)[:, :, j0 : j0 + width], res[:])
+                res = sb("res%d_%d" % (j0, u), [P, width], F32)
+                if last and u == 1:
+                    nc.vector.tensor_scalar_add(res[:], y[:, 0:width], bias[:, u : u + 1])
+                else:
+                    nc.scalar.activation(res[:], y[:, 0:width], IDENTITY, bias=bias[:, u : u + 1])
+                nc.sync.dma_start(out[cols, j0 : j0 + width], res[:])
 
-        for t in range(PACK):
-            max_abc(t, 0)
-            weigh(0, t)
-        round_h(0)
+        for s in range(2):
+            for kind in "bca":
+                first_pass(kind, s, 0)
+
         w2_bf = sb("w2_bf", [P, N * PACK], BF16)
-        nc.scalar.copy(
-            w2_bf[:].rearrange("p (c i t) -> p c t i", t=PACK, i=4),
-            w2_raw[:].rearrange("p t (c i) -> p c t i", i=4),
-        )
         w2_codes = sb("w2_codes", [P, N], U32)
         w2_plane = sb("w2_plane", [P, N], U8)
-        for t in range(PACK):
-            acc_b, acc_c = bank(t), bank(4 + t)
-            for a in range(PASSES):
-                b_pass(acc_b, t, a, 1)
-            for a in range(PASSES):
-                c_pass(acc_c, t, a, 1)
-            max_bc(acc_b, acc_c, t, 1)
-            max_abc(t, 1)
-        nc.vector.quantize_mx(out=w2_codes[:].bitcast(E4M3), scales=w2_plane[:], in_=w2_bf[:])
-        mix(0)
-        for c in range(1, len(CHUNKS)):
-            for t in range(PACK):
-                weigh(c, t)
-            round_h(c)
-            if c > 1:
-                mix(c - 1)
-        mix(len(CHUNKS) - 1)
+        h_bf0 = sb("h_bf0", [P, HALF * PACK], BF16)
+        for s in range(UNITS):
+            max_ab(s)
+            if s >= 1:
+                max_abc(s - 1)
+            if 2 <= s < 2 + PACK:
+                weigh(s - 2, 0, HALF)
+            elif s >= 2 + PACK:
+                weigh(s - 2, 0, QUARTER)
+                weigh(s - 2, QUARTER, QUARTER)
+            if s == 4:
+                interleave(nc.scalar.copy, w2_bf[:], w2_raw[:])
+                nc.vector.quantize_mx(out=w2_codes[:].bitcast(E4M3), scales=w2_plane[:], in_=w2_bf[:])
+            if s >= 6:
+                c0 = (s - 6) * QUARTER
+                interleave(
+                    nc.scalar.copy, h_bf0[:, c0 * PACK : (c0 + QUARTER) * PACK], h_first[:, :, c0 : c0 + QUARTER]
+                )
+        mix(0, HALF, h_bf0, 6, False)
+        max_abc(UNITS - 1)
+        h_bf1 = sb("h_bf1", [P, QUARTER * PACK], BF16)
+        h_bf2 = sb("h_bf2", [P, QUARTER * PACK], BF16)
+        for c0 in (0, QUARTER):
+            for s in (UNITS - 2, UNITS - 1):
+                weigh(s, c0, QUARTER)
+            if c0 == 0:
+                interleave(nc.scalar.copy, h_bf1[:], h_last[:, 0, :, :])
+        interleave(nc.scalar.copy, h_bf2[:, 0 : P * PACK], h_last[:, 1, :, 0:P])
+        mix(HALF, QUARTER, h_bf1, 0, False)
+        interleave(nc.vector.tensor_copy, h_bf2[:, P * PACK :], h_last[:, 1, :, P:])
+        mix(HALF + QUARTER, QUARTER, h_bf2, 2, True)

@@ -19,10 +19,11 @@ IDENTITY = mybir.ActivationFunctionType.Identity
 
 P = 128
 PACK = 4
+RUN = 8
 PASSES = K // (P * PACK)
 HALF = 512
-QUARTER = 256
 UNITS = PACK * S // HALF
+CHUNKS = ((0, 256), (256, 256), (512, 256), (768, 128), (896, 128))
 
 
 def tile_list_fresh_passage_banks_kernel(
@@ -45,6 +46,27 @@ def tile_list_fresh_passage_banks_kernel(
         def picks(j0, width):
             return offsets[:, j0 // 16 : (j0 + width) // 16]
 
+        tab_plane = sb("tab_plane", [P, T], U8)
+        for q in range(4):
+            nc.sync.dma_start(
+                tab_plane[32 * q + 24 : 32 * q + 32, :].bitcast(I32), tab_scales[:, 4 * q : 4 * q + 4, :].bitcast(I32)
+            )
+            nc.vector.memset(tab_plane[32 * q : 32 * q + 24, :].bitcast(I32), 0)
+        v_plane = sb("v_plane", [P, PASSES * S], U8)
+        nc.vector.memset(v_plane[:].bitcast(I32), 0)
+        w_plane = sb("w_plane", [P, PASSES, H // 4], I32)
+        nc.vector.memset(w_plane[:], 0)
+        w_plane_raw = sb("w_plane_raw", [P, PASSES * H], U8)
+
+        def load_w_scales(queue, row, scales):
+            for q in range(4):
+                queue.dma_start(
+                    w_plane_raw[32 * q + row : 32 * q + row + 4, :].bitcast(I32),
+                    scales[:, 4 * q : 4 * q + 4, :].rearrange("a r e -> r a e").bitcast(I32),
+                )
+
+        load_w_scales(nc.gpsimd, 0, wc_scales)
+
         tab_w, wa_raw, fresh = {}, {}, {}
 
         def load_tab(a, tag):
@@ -57,149 +79,132 @@ def tile_list_fresh_passage_banks_kernel(
 
         def load_fresh(t, tag):
             fresh[t] = sb("fresh%d" % t, [P, T], F32, tag)
-            nc.sync.dma_start(fresh[t][:], gT.rearrange("(p t) c -> t p c", t=PACK)[t])
-
-        def load_scales(queue, plane, row, scales):
-            for q in range(4):
-                queue.dma_start(
-                    plane[32 * q + row : 32 * q + row + 4, :].bitcast(I32),
-                    scales[:, 4 * q : 4 * q + 4, :].rearrange("a r e -> r a e").bitcast(I32),
-                )
-
-        tab_plane = sb("tab_plane", [P, PASSES * T], U8, "stage3")
-        nc.vector.memset(tab_plane[:].bitcast(I32), 0)
-        warm_in = sb("warm_in", [P, 1], F32, "stage5")
-        warm_out = sb("warm_out", [P, 1], F32, "stage4")
-        nc.vector.memset(warm_in[:], 0.0)
-        nc.scalar.activation(warm_out[:], warm_in[:], IDENTITY)
+            nc.sync.dma_start(fresh[t][:], gT.rearrange("(g t i) c -> t g i c", t=PACK, i=RUN)[t])
 
         load_tab(0, "stage0")
-        wb_raw = sb("wb_raw", [P, PASSES, H], I32, "stage1")
+        load_w_scales(nc.sync, 4, wb_scales)
+        load_wa(0, "stage1")
+        wb_raw = sb("wb_raw", [P, PASSES, H], I32, "stage2")
         nc.sync.dma_start(wb_raw[:], wb_words.rearrange("a p e i -> p a (e i)").bitcast(I32))
-        wc_raw = sb("wc_raw", [P, PASSES, H // 2], I32, "stage2")
+        wc_raw = sb("wc_raw", [P, PASSES, H // 2], I32, "stage3")
         nc.sync.dma_start(wc_raw[:], wc_words.rearrange("a p e -> p a e").bitcast(I32))
-        load_scales(nc.sync, tab_plane, 0, tab_scales)
-        load_wa(0, "stage4")
-        w_plane_raw = sb("w_plane_raw", [P, PASSES * H], U8, "stage5")
-        nc.gpsimd.memset(w_plane_raw[:].bitcast(I32), 0)
-        load_scales(nc.scalar, w_plane_raw, 4, wb_scales)
-        load_scales(nc.scalar, w_plane_raw, 0, wc_scales)
+        load_tab(1, "stage4")
 
-        v_codes, v_plane = {}, {}
+        picked_plane = sb("picked_plane", [P, S], U8)
+        nc.vector.tensor_copy(picked_plane[:], tab_plane[:].indirect(offsets[:]))
+        for a in range(PASSES):
+            nc.scalar.dma_start(
+                v_plane[0:100, a * S : (a + 1) * S].bitcast(I32), picked_plane[24 + 4 * a : 124 + 4 * a, :].bitcast(I32)
+            )
+
+        v_codes = {}
 
         def gather_codes(a, hf):
             v_codes[a, hf] = sb("v_codes%d_%d" % (a, hf), [P, HALF], U32)
             nc.vector.tensor_copy(v_codes[a, hf][:], tab_w[a][:].bitcast(U32).indirect(picks(hf * HALF, HALF)))
 
+        def deal(dealt, raw, words):
+            nc.vector.tensor_copy(
+                dealt.rearrange("p a (t g i) -> p a t g i", t=PACK, i=words),
+                raw.rearrange("p a (g t i) -> p a t g i", t=PACK, i=words),
+            )
+
+        wa_bf = [sb("wa_bf%d" % a, [P, H * PACK], BF16) for a in range(PASSES)]
+        wa_codes = [sb("wa_codes%d" % a, [P, H], U32) for a in range(PASSES)]
+        wa_plane = [sb("wa_plane%d" % a, [P, H], U8) for a in range(PASSES)]
+
+        def round_wa(a, t):
+            nc.scalar.copy(
+                wa_bf[a][:, t * H : (t + 1) * H].rearrange("p (g h j k) -> p g h k j", h=2, j=4, k=PACK),
+                wa_raw[a][:].rearrange("p k (g t h j) -> p t g h k j", t=PACK, h=2, j=4)[:, t],
+            )
+
+        def quantise_wa(a, t0, count):
+            cols = slice(t0 * P, (t0 + count) * P)
+            nc.vector.quantize_mx(
+                out=wa_codes[a][:, cols].bitcast(E4M3), scales=wa_plane[a][:, cols],
+                in_=wa_bf[a][:, t0 * H : (t0 + count) * H],
+            )
+
         gather_codes(0, 0)
         gather_codes(0, 1)
         load_wa(1, "stage0")
+        for q in range(4):
+            rows = slice(32 * q, 32 * q + 8)
+            deal(w_plane[rows], w_plane_raw[rows].bitcast(I32).rearrange("p (a e) -> p a e", a=PASSES), RUN // 4)
         wb_codes = sb("wb_codes", [P, PASSES, H], I32)
-        nc.vector.tensor_copy(
-            wb_codes[:].rearrange("p a (t m) -> p a m t", t=PACK),
-            wb_raw[:].rearrange("p a (m t) -> p a m t", t=PACK),
-        )
-        load_tab(1, "stage1")
-        wc_codes = sb("wc_codes", [P, PASSES, H], U16)
-        nc.vector.tensor_copy(
-            wc_codes[:].rearrange("p a (t m) -> p a m t", t=PACK),
-            wc_raw[:].bitcast(U16).rearrange("p a (m t) -> p a m t", t=PACK),
-        )
-        load_fresh(0, "stage2")
-        for a in range(PASSES):
-            v_plane[a] = sb("v_plane%d" % a, [P, S], U8)
-            nc.vector.tensor_copy(v_plane[a][:], tab_plane[:, a * T : (a + 1) * T].indirect(offsets[:]))
-        w_plane = sb("w_plane", [P, PASSES, H], U8)
-        nc.vector.tensor_copy(
-            w_plane[:].rearrange("p a (t m) -> p a m t", t=PACK),
-            w_plane_raw[:].rearrange("p (a m t) -> p a m t", a=PASSES, t=PACK),
-        )
-        load_fresh(1, "stage5")
-
-        wa_bf, wa_codes, wa_plane = {}, {}, {}
-
-        def round_wa(a):
-            wa_bf[a] = sb("wa_bf%d" % a, [P, H * PACK], BF16)
-            nc.scalar.copy(
-                wa_bf[a][:].rearrange("p (t m i) -> p m i t", t=PACK, i=PACK),
-                wa_raw[a][:].rearrange("p i (m t) -> p m i t", t=PACK),
-            )
-
-        def quantise_wa(a):
-            wa_codes[a] = sb("wa_codes%d" % a, [P, H], U32)
-            wa_plane[a] = sb("wa_plane%d" % a, [P, H], U8)
-            nc.vector.quantize_mx(out=wa_codes[a][:].bitcast(E4M3), scales=wa_plane[a][:], in_=wa_bf[a][:])
-
-        round_wa(0)
-        w2_raw = sb("w2_raw", [P, PACK, N], F32, "stage4")
-        nc.sync.dma_start(w2_raw[:], w2.rearrange("(p t) n -> p t n", t=PACK))
-        round_wa(1)
-        load_fresh(2, "stage0")
-        quantise_wa(0)
+        deal(wb_codes[:], wb_raw[:], RUN)
+        w2_raw = sb("w2_raw", [P, PACK, N], F32, "stage2")
+        for t in range(PACK):
+            nc.sync.dma_start(w2_raw[:, t, :], w2.rearrange("(g t i) n -> t g i n", t=PACK, i=RUN)[t])
+        wc_codes = sb("wc_codes", [P, PASSES, H // 2], I32)
+        deal(wc_codes[:], wc_raw[:], RUN // 2)
+        load_fresh(0, "stage3")
+        for t in range(PACK):
+            round_wa(0, t)
+        load_fresh(1, "stage1")
+        quantise_wa(0, 0, PACK)
         gather_codes(1, 0)
-        quantise_wa(1)
         gather_codes(1, 1)
-        load_fresh(3, "stage1")
-        bias = sb("bias", [P, N // P], F32, "stage3")
-        with nc.allow_non_contiguous_dma("one bias value for each partition"):
-            nc.sync.dma_start(bias[:], b2.rearrange("(u p) -> p u", p=P))
+        load_fresh(2, "stage4")
 
         def stationary(kind, a, t):
-            cols = slice(t * P, (t + 1) * P)
             if kind == "a":
+                cols = slice(t * P, (t + 1) * P)
                 return wa_codes[a][:, cols].bitcast(E4M3), wa_plane[a][:, cols]
+            plane_cols = slice(t * P // 4, (t + 1) * P // 4)
             if kind == "b":
-                return wb_codes[:, a, cols].bitcast(E4M3), w_plane[4:P, a, cols]
-            return wc_codes[:, a, cols].bitcast(E2M1), w_plane[:, a, cols]
+                return wb_codes[:, a, t * P : (t + 1) * P].bitcast(E4M3), w_plane[4:P, a, plane_cols].bitcast(U8)
+            return wc_codes[:, a, t * P // 2 : (t + 1) * P // 2].bitcast(E2M1), w_plane[:, a, plane_cols].bitcast(U8)
 
         acc = {}
 
         def first_pass(kind, s, a):
             hf, t = divmod(s, PACK)
             if a == 0:
-                acc[kind, s] = bank(2 * "abc".index(kind) + s % 2)
+                acc[kind, s] = bank(2 * t + ("abc".index(kind) // 2 + hf) % 2)
             codes, scales = stationary(kind, a, t)
+            moving_scales = v_plane[:, a * S + hf * HALF : a * S + (hf + 1) * HALF]
             nc.tensor.matmul_mx(
                 out=acc[kind, s][:], lhsT=codes, lhsT_scale=scales,
-                rhs=v_codes[a, hf][:].bitcast(E4M3), rhs_scale=v_plane[a][:, hf * HALF : (hf + 1) * HALF],
+                rhs=v_codes[a, hf][:].bitcast(E4M3), rhs_scale=moving_scales,
                 start=(a == 0), stop=(a == PASSES - 1),
             )
 
-        def first_product(kind, s):
-            for a in range(1 if s < 2 else 0, PASSES):
-                first_pass(kind, s, a)
+        best_bc, best = {}, {}
 
-        h_first = sb("h_first", [P, PACK, HALF], F32)
-        h_last = sb("h_last", [P, 2, PACK, QUARTER], F32)
-        h_last_flat = h_last[:].rearrange("p q t c -> p (q t c)")
-
-        def a_stage(s):
-            if 2 <= s < 2 + PACK:
-                return h_first[:, s - 2, :]
-            c0 = (s - 2 - PACK) % PACK * HALF
-            return h_last_flat[:, c0 : c0 + HALF]
-
-        best_ab, best = {}, {}
-
-        def max_ab(s):
-            a_sb = a_stage(s)
-            first_product("a", s)
-            nc.scalar.copy(a_sb, acc["a", s][:])
-            first_product("b", s)
-            best_ab[s] = sb("best_ab%d" % s, [P, HALF], F32)
-            nc.vector.tensor_tensor(best_ab[s][:], acc["b", s][:], a_sb, MAX)
+        def max_bc(s):
+            first = 1 if s < PACK else 0
+            for a in range(first, PASSES):
+                first_pass("b", s, a)
+            b_sb = sb("b_sb%d" % s, [P, HALF], F32)
+            nc.scalar.copy(b_sb[:], acc["b", s][:])
+            for a in range(first, PASSES):
+                first_pass("c", s, a)
+            best_bc[s] = sb("best_bc%d" % s, [P, HALF], F32)
+            nc.vector.tensor_tensor(best_bc[s][:], acc["c", s][:], b_sb[:], MAX)
 
         def max_abc(s):
-            first_product("c", s)
-            best[s] = sb("best%d" % s, [P, HALF], F32)
-            nc.vector.tensor_tensor(best[s][:], acc["c", s][:], best_ab[s][:], MAX)
+            for a in range(PASSES):
+                first_pass("a", s, a)
+            width = CHUNKS[0][1] if s == PACK - 1 else HALF
+            for c0 in range(0, HALF, width):
+                part = sb("best%d_%d" % (s, c0), [P, width], F32)
+                nc.vector.tensor_tensor(part[:], acc["a", s][:, c0 : c0 + width], best_bc[s][:, c0 : c0 + width], MAX)
+                best[s, c0] = part
 
-        def weigh(s, c0, width):
-            hf, t = divmod(s, PACK)
-            nc.vector.tensor_tensor(
-                h_last[:, c0 // QUARTER, t, :] if hf else h_first[:, t, :], fresh[t][:].indirect(picks(hf * HALF + c0, width)),
-                best[s][:, c0 : c0 + width], MULT,
-            )
+        h_f32 = {}
+
+        def h_chunk(j0, width):
+            if j0 < HALF:
+                return h_f32[0][:, :, j0 : j0 + width]
+            return h_f32[j0][:]
+
+        def weigh(t, j0, width):
+            hf, c0 = divmod(j0, HALF)
+            s = hf * PACK + t
+            chosen = best[s, c0][:, 0:width] if s == PACK - 1 else best[s, 0][:, c0 : c0 + width]
+            nc.vector.tensor_tensor(h_chunk(j0, width)[:, t, :], fresh[t][:].indirect(picks(j0, width)), chosen, MULT)
 
         def interleave(copy, dst, src):
             copy(
@@ -207,59 +212,71 @@ def tile_list_fresh_passage_banks_kernel(
                 src.rearrange("p t (c i) -> p c t i", i=4),
             )
 
-        def mix(j0, width, h_bf, bank0, last):
+        h_bf = {}
+
+        def round_h(j0, width, copy):
+            h_bf[j0] = sb("h_bf%d" % j0, [P, width * PACK], BF16)
+            interleave(copy, h_bf[j0][:], h_chunk(j0, width))
+
+        def mix(j0, width, banks, last):
             h_codes = sb("h_codes%d" % j0, [P, width], U32)
             h_plane = sb("h_plane%d" % j0, [P, width], U8)
-            nc.vector.quantize_mx(out=h_codes[:].bitcast(E4M3), scales=h_plane[:], in_=h_bf[:])
+            nc.vector.quantize_mx(out=h_codes[:].bitcast(E4M3), scales=h_plane[:], in_=h_bf[j0][:])
+            res = sb("res%d" % j0, [P, N // P, width], F32)
             for u in range(N // P):
-                y = bank(bank0 + u)
+                y = bank(banks[u])
                 cols = slice(u * P, (u + 1) * P)
                 nc.tensor.matmul_mx(
                     out=y[:, 0:width], lhsT=w2_codes[:, cols].bitcast(E4M3), lhsT_scale=w2_plane[:, cols],
                     rhs=h_codes[:].bitcast(E4M3), rhs_scale=h_plane[:], start=True, stop=True,
                 )
-                res = sb("res%d_%d" % (j0, u), [P, width], F32)
                 if last and u == 1:
-                    nc.vector.tensor_scalar_add(res[:], y[:, 0:width], bias[:, u : u + 1])
+                    nc.vector.tensor_scalar_add(res[:, u, :], y[:, 0:width], bias[:, u : u + 1])
                 else:
-                    nc.scalar.activation(res[:], y[:, 0:width], IDENTITY, bias=bias[:, u : u + 1])
-                nc.sync.dma_start(out[cols, j0 : j0 + width], res[:])
+                    nc.scalar.activation(res[:, u, :], y[:, 0:width], IDENTITY, bias=bias[:, u : u + 1])
+            nc.sync.dma_start(out[:, j0 : j0 + width].rearrange("(u p) j -> p u j", p=P), res[:])
 
-        for s in range(2):
-            for kind in "bca":
+        for s in range(PACK):
+            for kind in "bc":
                 first_pass(kind, s, 0)
-
+        for s in range(PACK):
+            max_bc(s)
+            round_wa(1, s)
+            if s % 2 == 1:
+                quantise_wa(1, s - 1, 2)
+        load_fresh(3, "stage0")
+        bias = sb("bias", [P, N // P], F32, "wa_bf0")
+        with nc.allow_non_contiguous_dma("one bias value for each partition"):
+            nc.sync.dma_start(bias[:], b2.rearrange("(u p) -> p u", p=P))
+        h_f32[0] = sb("h_first", [P, PACK, HALF], F32)
+        for s in range(PACK):
+            max_abc(s)
         w2_bf = sb("w2_bf", [P, N * PACK], BF16)
         w2_codes = sb("w2_codes", [P, N], U32)
         w2_plane = sb("w2_plane", [P, N], U8)
-        h_bf0 = sb("h_bf0", [P, HALF * PACK], BF16)
-        for s in range(UNITS):
-            max_ab(s)
-            if s >= 1:
-                max_abc(s - 1)
-            if 2 <= s < 2 + PACK:
-                weigh(s - 2, 0, HALF)
-            elif s >= 2 + PACK:
-                weigh(s - 2, 0, QUARTER)
-                weigh(s - 2, QUARTER, QUARTER)
-            if s == 4:
-                interleave(nc.scalar.copy, w2_bf[:], w2_raw[:])
-                nc.vector.quantize_mx(out=w2_codes[:].bitcast(E4M3), scales=w2_plane[:], in_=w2_bf[:])
-            if s >= 6:
-                c0 = (s - 6) * QUARTER
-                interleave(
-                    nc.scalar.copy, h_bf0[:, c0 * PACK : (c0 + QUARTER) * PACK], h_first[:, :, c0 : c0 + QUARTER]
-                )
-        mix(0, HALF, h_bf0, 6, False)
+        interleave(nc.scalar.copy, w2_bf[:], w2_raw[:])
+        nc.vector.quantize_mx(out=w2_codes[:].bitcast(E4M3), scales=w2_plane[:], in_=w2_bf[:])
+        for t in range(PACK):
+            max_bc(PACK + t)
+            if t >= 1:
+                max_abc(PACK + t - 1)
+            if t < PACK - 1:
+                weigh(t, 0, HALF)
         max_abc(UNITS - 1)
-        h_bf1 = sb("h_bf1", [P, QUARTER * PACK], BF16)
-        h_bf2 = sb("h_bf2", [P, QUARTER * PACK], BF16)
-        for c0 in (0, QUARTER):
-            for s in (UNITS - 2, UNITS - 1):
-                weigh(s, c0, QUARTER)
-            if c0 == 0:
-                interleave(nc.scalar.copy, h_bf1[:], h_last[:, 0, :, :])
-        interleave(nc.scalar.copy, h_bf2[:, 0 : P * PACK], h_last[:, 1, :, 0:P])
-        mix(HALF, QUARTER, h_bf1, 0, False)
-        interleave(nc.vector.tensor_copy, h_bf2[:, P * PACK :], h_last[:, 1, :, P:])
-        mix(HALF + QUARTER, QUARTER, h_bf2, 2, True)
+
+        for j0, width in CHUNKS[:2]:
+            weigh(PACK - 1, j0, width)
+            round_h(j0, width, nc.scalar.copy)
+        h_tags = ("best%d_0" % (PACK - 1), "h_first", "best%d_0" % (PACK - 1))
+        for c in range(2, len(CHUNKS)):
+            j0, width = CHUNKS[c]
+            h_f32[j0] = sb("h_f32_%d" % j0, [P, PACK, width], F32, h_tags[c - 2])
+            for t in range(PACK):
+                weigh(t, j0, width)
+            if c < len(CHUNKS) - 1:
+                round_h(j0, width, nc.scalar.copy)
+            if c == 2:
+                mix(CHUNKS[0][0], CHUNKS[0][1], (0, 1), False)
+            mix(CHUNKS[c - 1][0], CHUNKS[c - 1][1], (2 * c - 2, 2 * c - 1), False)
+        round_h(CHUNKS[-1][0], CHUNKS[-1][1], nc.vector.tensor_copy)
+        mix(CHUNKS[-1][0], CHUNKS[-1][1], (0, 1), True)

@@ -19,7 +19,6 @@ IDENTITY = mybir.ActivationFunctionType.Identity
 
 P = 128
 PACK = 4
-RUN = 8
 PASSES = K // (P * PACK)
 HALF = 512
 UNITS = PACK * S // HALF
@@ -47,25 +46,24 @@ def tile_list_fresh_passage_banks_kernel(
             return offsets[:, j0 // 16 : (j0 + width) // 16]
 
         tab_plane = sb("tab_plane", [P, T], U8)
-        for q in range(4):
+        nc.vector.memset(tab_plane[:].bitcast(I32), 0)
+        w_plane_raw = sb("w_plane_raw", [P, PASSES * H], U8, "stage5")
+        nc.vector.memset(w_plane_raw[:].bitcast(I32), 0)
+        v_plane_low = sb("v_plane_low", [P, S], U8)
+        nc.vector.memset(v_plane_low[:].bitcast(I32), 0)
+        wc_raw = sb("wc_raw", [P, PASSES, H // 2], I32, "stage3")
+        nc.sync.dma_start(wc_raw[:], wc_words.rearrange("a p e -> p a e").bitcast(I32))
+        for r in range(4):
             nc.sync.dma_start(
-                tab_plane[32 * q + 24 : 32 * q + 32, :].bitcast(I32), tab_scales[:, 4 * q : 4 * q + 4, :].bitcast(I32)
+                tab_plane[r:P:16, :].bitcast(I32), tab_scales.rearrange("a (q r) t -> r q a t", r=4)[r].bitcast(I32)
             )
-            nc.vector.memset(tab_plane[32 * q : 32 * q + 24, :].bitcast(I32), 0)
-        v_plane = sb("v_plane", [P, PASSES * S], U8)
-        nc.vector.memset(v_plane[:].bitcast(I32), 0)
-        w_plane = sb("w_plane", [P, PASSES, H // 4], I32)
-        nc.vector.memset(w_plane[:], 0)
-        w_plane_raw = sb("w_plane_raw", [P, PASSES * H], U8)
 
-        def load_w_scales(queue, row, scales):
+        def load_w_scales(row, scales):
             for q in range(4):
-                queue.dma_start(
+                nc.sync.dma_start(
                     w_plane_raw[32 * q + row : 32 * q + row + 4, :].bitcast(I32),
                     scales[:, 4 * q : 4 * q + 4, :].rearrange("a r e -> r a e").bitcast(I32),
                 )
-
-        load_w_scales(nc.gpsimd, 0, wc_scales)
 
         tab_w, wa_raw, fresh = {}, {}, {}
 
@@ -79,23 +77,20 @@ def tile_list_fresh_passage_banks_kernel(
 
         def load_fresh(t, tag):
             fresh[t] = sb("fresh%d" % t, [P, T], F32, tag)
-            nc.sync.dma_start(fresh[t][:], gT.rearrange("(g t i) c -> t g i c", t=PACK, i=RUN)[t])
+            nc.sync.dma_start(fresh[t][:], gT.rearrange("(p t) c -> t p c", t=PACK)[t])
 
         load_tab(0, "stage0")
-        load_w_scales(nc.sync, 4, wb_scales)
+        load_w_scales(4, wb_scales)
         load_wa(0, "stage1")
+        load_w_scales(0, wc_scales)
         wb_raw = sb("wb_raw", [P, PASSES, H], I32, "stage2")
         nc.sync.dma_start(wb_raw[:], wb_words.rearrange("a p e i -> p a (e i)").bitcast(I32))
-        wc_raw = sb("wc_raw", [P, PASSES, H // 2], I32, "stage3")
-        nc.sync.dma_start(wc_raw[:], wc_words.rearrange("a p e -> p a e").bitcast(I32))
         load_tab(1, "stage4")
 
         picked_plane = sb("picked_plane", [P, S], U8)
         nc.vector.tensor_copy(picked_plane[:], tab_plane[:].indirect(offsets[:]))
-        for a in range(PASSES):
-            nc.scalar.dma_start(
-                v_plane[0:100, a * S : (a + 1) * S].bitcast(I32), picked_plane[24 + 4 * a : 124 + 4 * a, :].bitcast(I32)
-            )
+        nc.sync.dma_start(v_plane_low[0:100, :].bitcast(I32), picked_plane[16:116, :].bitcast(I32))
+        v_plane = (picked_plane, v_plane_low)
 
         v_codes = {}
 
@@ -103,20 +98,19 @@ def tile_list_fresh_passage_banks_kernel(
             v_codes[a, hf] = sb("v_codes%d_%d" % (a, hf), [P, HALF], U32)
             nc.vector.tensor_copy(v_codes[a, hf][:], tab_w[a][:].bitcast(U32).indirect(picks(hf * HALF, HALF)))
 
-        def deal(dealt, raw, words):
+        def deal(dealt, raw):
             nc.vector.tensor_copy(
-                dealt.rearrange("p a (t g i) -> p a t g i", t=PACK, i=words),
-                raw.rearrange("p a (g t i) -> p a t g i", t=PACK, i=words),
+                dealt.rearrange("p a (t m) -> p a m t", t=PACK), raw.rearrange("p a (m t) -> p a m t", t=PACK)
             )
 
         wa_bf = [sb("wa_bf%d" % a, [P, H * PACK], BF16) for a in range(PASSES)]
         wa_codes = [sb("wa_codes%d" % a, [P, H], U32) for a in range(PASSES)]
         wa_plane = [sb("wa_plane%d" % a, [P, H], U8) for a in range(PASSES)]
 
-        def round_wa(a, t):
+        def round_wa(a, t0, count):
             nc.scalar.copy(
-                wa_bf[a][:, t * H : (t + 1) * H].rearrange("p (g h j k) -> p g h k j", h=2, j=4, k=PACK),
-                wa_raw[a][:].rearrange("p k (g t h j) -> p t g h k j", t=PACK, h=2, j=4)[:, t],
+                wa_bf[a][:].rearrange("p (t m k) -> p m k t", t=PACK, k=PACK)[:, :, :, t0 : t0 + count],
+                wa_raw[a][:].rearrange("p k (m t) -> p m k t", t=PACK)[:, :, :, t0 : t0 + count],
             )
 
         def quantise_wa(a, t0, count):
@@ -129,19 +123,16 @@ def tile_list_fresh_passage_banks_kernel(
         gather_codes(0, 0)
         gather_codes(0, 1)
         load_wa(1, "stage0")
-        for q in range(4):
-            rows = slice(32 * q, 32 * q + 8)
-            deal(w_plane[rows], w_plane_raw[rows].bitcast(I32).rearrange("p (a e) -> p a e", a=PASSES), RUN // 4)
+        w_plane = sb("w_plane", [P, PASSES, H], U8)
+        deal(w_plane[:], w_plane_raw[:].rearrange("p (a e) -> p a e", a=PASSES))
         wb_codes = sb("wb_codes", [P, PASSES, H], I32)
-        deal(wb_codes[:], wb_raw[:], RUN)
-        w2_raw = sb("w2_raw", [P, PACK, N], F32, "stage2")
-        for t in range(PACK):
-            nc.sync.dma_start(w2_raw[:, t, :], w2.rearrange("(g t i) n -> t g i n", t=PACK, i=RUN)[t])
-        wc_codes = sb("wc_codes", [P, PASSES, H // 2], I32)
-        deal(wc_codes[:], wc_raw[:], RUN // 2)
-        load_fresh(0, "stage3")
-        for t in range(PACK):
-            round_wa(0, t)
+        deal(wb_codes[:], wb_raw[:])
+        w2_raw = sb("w2_raw", [P, PACK, N], F32, "stage5")
+        nc.sync.dma_start(w2_raw[:], w2.rearrange("(p t) n -> p t n", t=PACK))
+        wc_codes = sb("wc_codes", [P, PASSES, H], U16)
+        deal(wc_codes[:], wc_raw[:].bitcast(U16))
+        load_fresh(0, "stage2")
+        round_wa(0, 0, PACK)
         load_fresh(1, "stage1")
         quantise_wa(0, 0, PACK)
         gather_codes(1, 0)
@@ -149,13 +140,12 @@ def tile_list_fresh_passage_banks_kernel(
         load_fresh(2, "stage4")
 
         def stationary(kind, a, t):
+            cols = slice(t * P, (t + 1) * P)
             if kind == "a":
-                cols = slice(t * P, (t + 1) * P)
                 return wa_codes[a][:, cols].bitcast(E4M3), wa_plane[a][:, cols]
-            plane_cols = slice(t * P // 4, (t + 1) * P // 4)
             if kind == "b":
-                return wb_codes[:, a, t * P : (t + 1) * P].bitcast(E4M3), w_plane[4:P, a, plane_cols].bitcast(U8)
-            return wc_codes[:, a, t * P // 2 : (t + 1) * P // 2].bitcast(E2M1), w_plane[:, a, plane_cols].bitcast(U8)
+                return wb_codes[:, a, cols].bitcast(E4M3), w_plane[4:P, a, cols]
+            return wc_codes[:, a, cols].bitcast(E2M1), w_plane[:, a, cols]
 
         acc = {}
 
@@ -164,7 +154,7 @@ def tile_list_fresh_passage_banks_kernel(
             if a == 0:
                 acc[kind, s] = bank(2 * t + ("abc".index(kind) // 2 + hf) % 2)
             codes, scales = stationary(kind, a, t)
-            moving_scales = v_plane[:, a * S + hf * HALF : a * S + (hf + 1) * HALF]
+            moving_scales = v_plane[a][:, hf * HALF : (hf + 1) * HALF]
             nc.tensor.matmul_mx(
                 out=acc[kind, s][:], lhsT=codes, lhsT_scale=scales,
                 rhs=v_codes[a, hf][:].bitcast(E4M3), rhs_scale=moving_scales,
@@ -241,8 +231,8 @@ def tile_list_fresh_passage_banks_kernel(
                 first_pass(kind, s, 0)
         for s in range(PACK):
             max_bc(s)
-            round_wa(1, s)
             if s % 2 == 1:
+                round_wa(1, s - 1, 2)
                 quantise_wa(1, s - 1, 2)
         load_fresh(3, "stage0")
         bias = sb("bias", [P, N // P], F32, "wa_bf0")

@@ -23,6 +23,7 @@ PASSES = K // (P * PACK)
 HALF = 512
 UNITS = PACK * S // HALF
 CHUNKS = ((0, 256), (256, 256), (512, 256), (768, 128), (896, 128))
+BANKS = {"a": (2, 4, 6, 3, 5, 7, 0, 1), "b": (0, 2, 4, 6, 0, 2, 6, 5), "c": (1, 3, 5, 7, 1, 4, 3, 7)}
 
 
 def tile_list_fresh_passage_banks_kernel(
@@ -36,8 +37,8 @@ def tile_list_fresh_passage_banks_kernel(
         def sb(name, shape, dtype, tag=""):
             return keep.tile(shape, dtype, name=name, tag=tag or name, align_bytes=64)
 
-        def bank(i):
-            return psum.tile([P, HALF], F32, name="bank%d" % i)
+        def bank(name, i):
+            return psum.tile([P, HALF], F32, name=name, offset=2048 * i)
 
         offsets = keep.tile([P, S // 16], U16, name="offsets")
         nc.sync.dma_start(offsets[:], offs)
@@ -46,12 +47,12 @@ def tile_list_fresh_passage_banks_kernel(
             return offsets[:, j0 // 16 : (j0 + width) // 16]
 
         tab_plane = sb("tab_plane", [P, T], U8)
-        nc.vector.memset(tab_plane[:].bitcast(I32), 0)
-        w_plane_raw = sb("w_plane_raw", [P, PASSES * H], U8, "stage5")
+        nc.gpsimd.memset(tab_plane[:].bitcast(I32), 0)
+        w_plane_raw = sb("w_plane_raw", [P, PASSES * H], U8)
         nc.vector.memset(w_plane_raw[:].bitcast(I32), 0)
         v_plane_low = sb("v_plane_low", [P, S], U8)
         nc.vector.memset(v_plane_low[:].bitcast(I32), 0)
-        wc_raw = sb("wc_raw", [P, PASSES, H // 2], I32, "stage3")
+        wc_raw = sb("wc_raw", [P, PASSES, H // 2], I32)
         nc.sync.dma_start(wc_raw[:], wc_words.rearrange("a p e -> p a e").bitcast(I32))
         for r in range(4):
             nc.sync.dma_start(
@@ -67,41 +68,42 @@ def tile_list_fresh_passage_banks_kernel(
 
         tab_w, wa_raw, fresh = {}, {}, {}
 
-        def load_tab(a, tag):
-            tab_w[a] = sb("tab_w%d" % a, [P, T], I32, tag)
+        def load_tab(a):
+            tab_w[a] = sb("tab_w%d" % a, [P, T], I32)
             nc.sync.dma_start(tab_w[a][:], tab_words[a].rearrange("p t i -> p (t i)").bitcast(I32))
 
-        def load_wa(a, tag):
-            wa_raw[a] = sb("wa_raw%d" % a, [P, PACK, H], F32, tag)
+        def load_wa(a):
+            wa_raw[a] = sb("wa_raw%d" % a, [P, PACK, H], F32)
             nc.sync.dma_start(wa_raw[a][:], wa[512 * a : 512 * (a + 1), :].rearrange("(p i) e -> p i e", i=PACK))
 
-        def load_fresh(t, tag):
-            fresh[t] = sb("fresh%d" % t, [P, T], F32, tag)
+        def load_fresh(t):
+            fresh[t] = sb("fresh%d" % t, [P, T], F32)
             nc.sync.dma_start(fresh[t][:], gT.rearrange("(p t) c -> t p c", t=PACK)[t])
 
-        load_tab(0, "stage0")
+        load_tab(0)
         load_w_scales(4, wb_scales)
-        load_wa(0, "stage1")
+        load_wa(0)
         load_w_scales(0, wc_scales)
-        wb_raw = sb("wb_raw", [P, PASSES, H], I32, "stage2")
+        wb_raw = sb("wb_raw", [P, PASSES, H], I32)
         nc.sync.dma_start(wb_raw[:], wb_words.rearrange("a p e i -> p a (e i)").bitcast(I32))
-        load_tab(1, "stage4")
 
+        def deal(dealt, raw, order):
+            nc.vector.tensor_copy(
+                dealt.rearrange("p a (t m) -> " + order, t=PACK), raw.rearrange("p a (m t) -> " + order, t=PACK)
+            )
+
+        wc_codes = sb("wc_codes", [P, PASSES, H], U16)
+        deal(wc_codes[:], wc_raw[:].bitcast(U16), "p a t m")
         picked_plane = sb("picked_plane", [P, S], U8)
         nc.vector.tensor_copy(picked_plane[:], tab_plane[:].indirect(offsets[:]))
         nc.sync.dma_start(v_plane_low[0:100, :].bitcast(I32), picked_plane[16:116, :].bitcast(I32))
+        load_tab(1)
         v_plane = (picked_plane, v_plane_low)
 
-        v_codes = {}
+        v_codes = [sb("v_codes%d" % a, [P, S], U32) for a in range(PASSES)]
 
-        def gather_codes(a, hf):
-            v_codes[a, hf] = sb("v_codes%d_%d" % (a, hf), [P, HALF], U32)
-            nc.vector.tensor_copy(v_codes[a, hf][:], tab_w[a][:].bitcast(U32).indirect(picks(hf * HALF, HALF)))
-
-        def deal(dealt, raw):
-            nc.vector.tensor_copy(
-                dealt.rearrange("p a (t m) -> p a m t", t=PACK), raw.rearrange("p a (m t) -> p a m t", t=PACK)
-            )
+        def gather_codes(a, j0, width):
+            nc.vector.tensor_copy(v_codes[a][:, j0 : j0 + width], tab_w[a][:].bitcast(U32).indirect(picks(j0, width)))
 
         wa_bf = [sb("wa_bf%d" % a, [P, H * PACK], BF16) for a in range(PASSES)]
         wa_codes = [sb("wa_codes%d" % a, [P, H], U32) for a in range(PASSES)]
@@ -120,24 +122,22 @@ def tile_list_fresh_passage_banks_kernel(
                 in_=wa_bf[a][:, t0 * H : (t0 + count) * H],
             )
 
-        gather_codes(0, 0)
-        gather_codes(0, 1)
-        load_wa(1, "stage0")
+        gather_codes(0, 0, S)
+        load_wa(1)
         w_plane = sb("w_plane", [P, PASSES, H], U8)
-        deal(w_plane[:], w_plane_raw[:].rearrange("p (a e) -> p a e", a=PASSES))
+        deal(w_plane[:], w_plane_raw[:].rearrange("p (a e) -> p a e", a=PASSES), "p a t m")
         wb_codes = sb("wb_codes", [P, PASSES, H], I32)
-        deal(wb_codes[:], wb_raw[:])
-        w2_raw = sb("w2_raw", [P, PACK, N], F32, "stage5")
+        deal(wb_codes[:], wb_raw[:], "p a m t")
+        load_fresh(0)
+        round_wa(0, 0, 2)
+        round_wa(0, 2, 2)
+        load_fresh(1)
+        w2_raw = sb("w2_raw", [P, PACK, N], F32)
         nc.sync.dma_start(w2_raw[:], w2.rearrange("(p t) n -> p t n", t=PACK))
-        wc_codes = sb("wc_codes", [P, PASSES, H], U16)
-        deal(wc_codes[:], wc_raw[:].bitcast(U16))
-        load_fresh(0, "stage2")
-        round_wa(0, 0, PACK)
-        load_fresh(1, "stage1")
         quantise_wa(0, 0, PACK)
-        gather_codes(1, 0)
-        gather_codes(1, 1)
-        load_fresh(2, "stage4")
+        gather_codes(1, 0, HALF)
+        gather_codes(1, HALF, HALF)
+        load_fresh(2)
 
         def stationary(kind, a, t):
             cols = slice(t * P, (t + 1) * P)
@@ -152,12 +152,12 @@ def tile_list_fresh_passage_banks_kernel(
         def first_pass(kind, s, a):
             hf, t = divmod(s, PACK)
             if a == 0:
-                acc[kind, s] = bank(2 * t + ("abc".index(kind) // 2 + hf) % 2)
+                acc[kind, s] = bank("acc_%s%d" % (kind, s), BANKS[kind][s])
             codes, scales = stationary(kind, a, t)
             moving_scales = v_plane[a][:, hf * HALF : (hf + 1) * HALF]
             nc.tensor.matmul_mx(
                 out=acc[kind, s][:], lhsT=codes, lhsT_scale=scales,
-                rhs=v_codes[a, hf][:].bitcast(E4M3), rhs_scale=moving_scales,
+                rhs=v_codes[a][:, hf * HALF : (hf + 1) * HALF].bitcast(E4M3), rhs_scale=moving_scales,
                 start=(a == 0), stop=(a == PASSES - 1),
             )
 
@@ -214,7 +214,7 @@ def tile_list_fresh_passage_banks_kernel(
             nc.vector.quantize_mx(out=h_codes[:].bitcast(E4M3), scales=h_plane[:], in_=h_bf[j0][:])
             res = sb("res%d" % j0, [P, N // P, width], F32)
             for u in range(N // P):
-                y = bank(banks[u])
+                y = bank("y%d_%d" % (j0, u), banks[u])
                 cols = slice(u * P, (u + 1) * P)
                 nc.tensor.matmul_mx(
                     out=y[:, 0:width], lhsT=w2_codes[:, cols].bitcast(E4M3), lhsT_scale=w2_plane[:, cols],
@@ -234,26 +234,31 @@ def tile_list_fresh_passage_banks_kernel(
             if s % 2 == 1:
                 round_wa(1, s - 1, 2)
                 quantise_wa(1, s - 1, 2)
-        load_fresh(3, "stage0")
-        bias = sb("bias", [P, N // P], F32, "wa_bf0")
+        load_fresh(3)
+        bias = sb("bias", [P, N // P], F32)
         with nc.allow_non_contiguous_dma("one bias value for each partition"):
             nc.sync.dma_start(bias[:], b2.rearrange("(u p) -> p u", p=P))
         h_f32[0] = sb("h_first", [P, PACK, HALF], F32)
-        for s in range(PACK):
-            max_abc(s)
         w2_bf = sb("w2_bf", [P, N * PACK], BF16)
         w2_codes = sb("w2_codes", [P, N], U32)
         w2_plane = sb("w2_plane", [P, N], U8)
         interleave(nc.scalar.copy, w2_bf[:], w2_raw[:])
         nc.vector.quantize_mx(out=w2_codes[:].bitcast(E4M3), scales=w2_plane[:], in_=w2_bf[:])
-        for t in range(PACK):
-            max_bc(PACK + t)
-            if t >= 1:
-                max_abc(PACK + t - 1)
-            if t < PACK - 1:
-                weigh(t, 0, HALF)
-        max_abc(UNITS - 1)
-
+        max_bc(4)
+        max_abc(0)
+        max_abc(1)
+        weigh(0, 0, HALF)
+        max_abc(4)
+        max_bc(5)
+        max_abc(2)
+        max_abc(3)
+        weigh(1, 0, HALF)
+        max_abc(5)
+        max_bc(6)
+        weigh(2, 0, HALF)
+        max_bc(7)
+        max_abc(6)
+        max_abc(7)
         for j0, width in CHUNKS[:2]:
             weigh(PACK - 1, j0, width)
             round_h(j0, width, nc.scalar.copy)

@@ -24,6 +24,7 @@ HALF = 512
 UNITS = PACK * S // HALF
 CHUNKS = ((0, 256), (256, 256), (512, 256), (768, 128), (896, 128))
 BANKS = {"a": (2, 4, 6, 3, 5, 7, 0, 1), "b": (0, 2, 4, 6, 0, 2, 6, 5), "c": (1, 3, 5, 7, 1, 4, 3, 7)}
+LIVE = 96
 
 
 def tile_list_fresh_passage_banks_kernel(
@@ -47,24 +48,18 @@ def tile_list_fresh_passage_banks_kernel(
             return offsets[:, j0 // 16 : (j0 + width) // 16]
 
         tab_plane = sb("tab_plane", [P, T], U8)
-        nc.gpsimd.memset(tab_plane[:].bitcast(I32), 0)
+        nc.sync.dma_start(tab_plane[LIVE:P, :].bitcast(I32), tab_scales.rearrange("a q t -> q a t").bitcast(I32))
         w_plane_raw = sb("w_plane_raw", [P, PASSES * H], U8)
         nc.vector.memset(w_plane_raw[:].bitcast(I32), 0)
-        v_plane_low = sb("v_plane_low", [P, S], U8)
-        nc.vector.memset(v_plane_low[:].bitcast(I32), 0)
-        wc_raw = sb("wc_raw", [P, PASSES, H // 2], I32)
-        nc.sync.dma_start(wc_raw[:], wc_words.rearrange("a p e -> p a e").bitcast(I32))
-        for r in range(4):
-            nc.sync.dma_start(
-                tab_plane[r:P:16, :].bitcast(I32), tab_scales.rearrange("a (q r) t -> r q a t", r=4)[r].bitcast(I32)
-            )
+        nc.vector.memset(tab_plane[0:LIVE, :].bitcast(I32), 0)
+        v_planes = sb("v_planes", [P, PASSES * S], U8)
+        nc.vector.memset(v_planes[:].bitcast(I32), 0)
 
-        def load_w_scales(row, scales):
-            for q in range(4):
-                nc.sync.dma_start(
-                    w_plane_raw[32 * q + row : 32 * q + row + 4, :].bitcast(I32),
-                    scales[:, 4 * q : 4 * q + 4, :].rearrange("a r e -> r a e").bitcast(I32),
-                )
+        def load_w_scales(engine, row, scales, q):
+            engine.dma_start(
+                w_plane_raw[32 * q + row : 32 * q + row + 4, :].bitcast(I32),
+                scales[:, 4 * q : 4 * q + 4, :].rearrange("a r e -> r a e").bitcast(I32),
+            )
 
         tab_w, wa_raw, fresh = {}, {}, {}
 
@@ -81,24 +76,32 @@ def tile_list_fresh_passage_banks_kernel(
             nc.sync.dma_start(fresh[t][:], gT.rearrange("(p t) c -> t p c", t=PACK)[t])
 
         load_tab(0)
-        load_w_scales(4, wb_scales)
+        wc_raw = sb("wc_raw", [P, PASSES, H // 2], I32)
+        nc.sync.dma_start(wc_raw[:], wc_words.rearrange("a p e -> p a e").bitcast(I32))
+        for q in range(2):
+            load_w_scales(nc.gpsimd, 0, wc_scales, q)
+        for q in range(4):
+            load_w_scales(nc.sync, 4, wb_scales, q)
+        load_w_scales(nc.sync, 0, wc_scales, 2)
         load_wa(0)
-        load_w_scales(0, wc_scales)
-        wb_raw = sb("wb_raw", [P, PASSES, H], I32)
-        nc.sync.dma_start(wb_raw[:], wb_words.rearrange("a p e i -> p a (e i)").bitcast(I32))
+        load_w_scales(nc.sync, 0, wc_scales, 3)
 
         def deal(dealt, raw, order):
             nc.vector.tensor_copy(
                 dealt.rearrange("p a (t m) -> " + order, t=PACK), raw.rearrange("p a (m t) -> " + order, t=PACK)
             )
 
-        wc_codes = sb("wc_codes", [P, PASSES, H], U16)
-        deal(wc_codes[:], wc_raw[:].bitcast(U16), "p a t m")
         picked_plane = sb("picked_plane", [P, S], U8)
         nc.vector.tensor_copy(picked_plane[:], tab_plane[:].indirect(offsets[:]))
-        nc.sync.dma_start(v_plane_low[0:100, :].bitcast(I32), picked_plane[16:116, :].bitcast(I32))
+        for q in range(4):
+            nc.sync.dma_start(
+                v_planes[32 * q : 32 * q + 4, :].bitcast(I32).rearrange("r (a j) -> r a j", a=PASSES),
+                picked_plane[LIVE + 8 * q : LIVE + 8 * q + 8, :].bitcast(I32),
+            )
+        wb_raw = sb("wb_raw", [P, PASSES, H], I32)
+        nc.sync.dma_start(wb_raw[:], wb_words.rearrange("a p e i -> p a (e i)").bitcast(I32))
         load_tab(1)
-        v_plane = (picked_plane, v_plane_low)
+        v_plane = [v_planes[:, a * S : (a + 1) * S] for a in range(PASSES)]
 
         v_codes = [sb("v_codes%d" % a, [P, S], U32) for a in range(PASSES)]
 
@@ -124,6 +127,8 @@ def tile_list_fresh_passage_banks_kernel(
 
         gather_codes(0, 0, S)
         load_wa(1)
+        wc_codes = sb("wc_codes", [P, PASSES, H], U16)
+        deal(wc_codes[:], wc_raw[:].bitcast(U16), "p a t m")
         w_plane = sb("w_plane", [P, PASSES, H], U8)
         deal(w_plane[:], w_plane_raw[:].rearrange("p (a e) -> p a e", a=PASSES), "p a t m")
         wb_codes = sb("wb_codes", [P, PASSES, H], I32)

@@ -23,8 +23,9 @@ PASSES = K // (P * PACK)
 HALF = 512
 UNITS = PACK * S // HALF
 CHUNKS = ((0, 256), (256, 256), (512, 256), (768, 128), (896, 128))
-BANKS = {"a": (2, 4, 6, 3, 5, 7, 0, 1), "b": (0, 2, 4, 6, 0, 2, 6, 5), "c": (1, 3, 5, 7, 1, 4, 3, 7)}
+BANKS = {"a": (2, 3, 6, 7, 1, 5, 0, 4), "b": (4, 5, 6, 7, 4, 3, 5, 7), "c": (0, 1, 0, 1, 0, 2, 1, 6)}
 LIVE = 96
+STAGE = 64
 
 
 def tile_list_fresh_passage_banks_kernel(
@@ -33,6 +34,7 @@ def tile_list_fresh_passage_banks_kernel(
     nc = tc.nc
     with ExitStack() as ctx:
         keep = ctx.enter_context(tc.tile_pool(name="keep", bufs=1))
+        shared = ctx.enter_context(tc.tile_pool(name="shared", bufs=1))
         psum = ctx.enter_context(tc.psum_pool(name="psum", bufs=1))
 
         def sb(name, shape, dtype, tag=""):
@@ -47,19 +49,19 @@ def tile_list_fresh_passage_banks_kernel(
         def picks(j0, width):
             return offsets[:, j0 // 16 : (j0 + width) // 16]
 
+        w_rows = sb("w_rows", [P, H], U8)
+        for w, scales in enumerate((wc_scales, wb_scales)):
+            nc.sync.dma_start(
+                w_rows[STAGE + w : P : 2, :].bitcast(I32), scales.rearrange("a q e -> q a e").bitcast(I32)
+            )
         tab_plane = sb("tab_plane", [P, T], U8)
         nc.sync.dma_start(tab_plane[LIVE:P, :].bitcast(I32), tab_scales.rearrange("a q t -> q a t").bitcast(I32))
-        w_plane_raw = sb("w_plane_raw", [P, PASSES * H], U8)
-        nc.vector.memset(w_plane_raw[:].bitcast(I32), 0)
+        nc.vector.memset(w_rows[0:STAGE, :].bitcast(I32), 0)
         nc.vector.memset(tab_plane[0:LIVE, :].bitcast(I32), 0)
+        w_planes = sb("w_planes", [P, 2 * PASSES * H], U8)
+        nc.vector.memset(w_planes[:].bitcast(I32), 0)
         v_planes = sb("v_planes", [P, PASSES * S], U8)
         nc.vector.memset(v_planes[:].bitcast(I32), 0)
-
-        def load_w_scales(engine, row, scales, q):
-            engine.dma_start(
-                w_plane_raw[32 * q + row : 32 * q + row + 4, :].bitcast(I32),
-                scales[:, 4 * q : 4 * q + 4, :].rearrange("a r e -> r a e").bitcast(I32),
-            )
 
         tab_w, wa_raw, fresh = {}, {}, {}
 
@@ -78,19 +80,18 @@ def tile_list_fresh_passage_banks_kernel(
         load_tab(0)
         wc_raw = sb("wc_raw", [P, PASSES, H // 2], I32)
         nc.sync.dma_start(wc_raw[:], wc_words.rearrange("a p e -> p a e").bitcast(I32))
-        for q in range(2):
-            load_w_scales(nc.gpsimd, 0, wc_scales, q)
+
+        def deal(copy, dealt, raw, order):
+            copy(dealt.rearrange("p (t m) -> " + order, t=PACK), raw.rearrange("p (m t) -> " + order, t=PACK))
+
+        w_rows_dealt = sb("w_rows_dealt", [P, H], U8)
+        deal(nc.vector.tensor_copy, w_rows_dealt[:], w_rows[:], "p t m")
         for q in range(4):
-            load_w_scales(nc.sync, 4, wb_scales, q)
-        load_w_scales(nc.sync, 0, wc_scales, 2)
-        load_wa(0)
-        load_w_scales(nc.sync, 0, wc_scales, 3)
-
-        def deal(dealt, raw, order):
-            nc.vector.tensor_copy(
-                dealt.rearrange("p a (t m) -> " + order, t=PACK), raw.rearrange("p a (m t) -> " + order, t=PACK)
+            nc.sync.dma_start(
+                w_planes[32 * q : 32 * q + 4, :].bitcast(I32).rearrange("r (x e) -> r x e", x=2 * PASSES),
+                w_rows_dealt[STAGE + 16 * q : STAGE + 16 * q + 16, :].bitcast(I32),
             )
-
+        load_tab(1)
         picked_plane = sb("picked_plane", [P, S], U8)
         nc.vector.tensor_copy(picked_plane[:], tab_plane[:].indirect(offsets[:]))
         for q in range(4):
@@ -98,9 +99,19 @@ def tile_list_fresh_passage_banks_kernel(
                 v_planes[32 * q : 32 * q + 4, :].bitcast(I32).rearrange("r (a j) -> r a j", a=PASSES),
                 picked_plane[LIVE + 8 * q : LIVE + 8 * q + 8, :].bitcast(I32),
             )
-        wb_raw = sb("wb_raw", [P, PASSES, H], I32)
+        wb_raw = shared.tile([P, PASSES, H], I32, name="wb_raw", offset=0)
         nc.sync.dma_start(wb_raw[:], wb_words.rearrange("a p e i -> p a (e i)").bitcast(I32))
-        load_tab(1)
+        load_wa(0)
+        load_wa(1)
+        load_fresh(0)
+        load_fresh(1)
+        w2_raw = sb("w2_raw", [P, PACK, N], F32)
+        nc.sync.dma_start(w2_raw[:], w2.rearrange("(p t) n -> p t n", t=PACK))
+        load_fresh(2)
+        load_fresh(3)
+        bias = sb("bias", [P, N // P], F32)
+        with nc.allow_non_contiguous_dma("one bias value for each partition"):
+            nc.sync.dma_start(bias[:], b2.rearrange("(u p) -> p u", p=P))
         v_plane = [v_planes[:, a * S : (a + 1) * S] for a in range(PASSES)]
 
         v_codes = [sb("v_codes%d" % a, [P, S], U32) for a in range(PASSES)]
@@ -112,8 +123,8 @@ def tile_list_fresh_passage_banks_kernel(
         wa_codes = [sb("wa_codes%d" % a, [P, H], U32) for a in range(PASSES)]
         wa_plane = [sb("wa_plane%d" % a, [P, H], U8) for a in range(PASSES)]
 
-        def round_wa(a, t0, count):
-            nc.scalar.copy(
+        def round_wa(a, t0, count, copy):
+            copy(
                 wa_bf[a][:].rearrange("p (t m k) -> p m k t", t=PACK, k=PACK)[:, :, :, t0 : t0 + count],
                 wa_raw[a][:].rearrange("p k (m t) -> p m k t", t=PACK)[:, :, :, t0 : t0 + count],
             )
@@ -125,32 +136,27 @@ def tile_list_fresh_passage_banks_kernel(
                 in_=wa_bf[a][:, t0 * H : (t0 + count) * H],
             )
 
-        gather_codes(0, 0, S)
-        load_wa(1)
-        wc_codes = sb("wc_codes", [P, PASSES, H], U16)
-        deal(wc_codes[:], wc_raw[:].bitcast(U16), "p a t m")
-        w_plane = sb("w_plane", [P, PASSES, H], U8)
-        deal(w_plane[:], w_plane_raw[:].rearrange("p (a e) -> p a e", a=PASSES), "p a t m")
-        wb_codes = sb("wb_codes", [P, PASSES, H], I32)
-        deal(wb_codes[:], wb_raw[:], "p a m t")
-        load_fresh(0)
-        round_wa(0, 0, 2)
-        round_wa(0, 2, 2)
-        load_fresh(1)
-        w2_raw = sb("w2_raw", [P, PACK, N], F32)
-        nc.sync.dma_start(w2_raw[:], w2.rearrange("(p t) n -> p t n", t=PACK))
-        quantise_wa(0, 0, PACK)
-        gather_codes(1, 0, HALF)
-        gather_codes(1, HALF, HALF)
-        load_fresh(2)
+        wc_codes = [sb("wc_codes%d" % a, [P, H], U16) for a in range(PASSES)]
+        wb_codes = sb("wb_codes", [P, PASSES, H], U32)
+        for a in range(PASSES):
+            deal(nc.scalar.copy, wc_codes[a][:], wc_raw[:, a, :].bitcast(U16), "p t m")
+        for a in range(PASSES):
+            gather_codes(a, 0, HALF)
+            gather_codes(a, HALF, HALF)
+        nc.scalar.copy(
+            wb_codes[:].rearrange("p a (t m) -> p a m t", t=PACK),
+            wb_raw[:].bitcast(U32).rearrange("p a (m t) -> p a m t", t=PACK),
+        )
 
         def stationary(kind, a, t):
             cols = slice(t * P, (t + 1) * P)
             if kind == "a":
                 return wa_codes[a][:, cols].bitcast(E4M3), wa_plane[a][:, cols]
+            w = 1 if kind == "b" else 0
+            e0 = (2 * a + w) * H + t * P
             if kind == "b":
-                return wb_codes[:, a, cols].bitcast(E4M3), w_plane[4:P, a, cols]
-            return wc_codes[:, a, cols].bitcast(E2M1), w_plane[:, a, cols]
+                return wb_codes[:, a, cols].bitcast(E4M3), w_planes[:, e0 : e0 + P]
+            return wc_codes[a][:, cols].bitcast(E2M1), w_planes[:, e0 : e0 + P]
 
         acc = {}
 
@@ -168,16 +174,25 @@ def tile_list_fresh_passage_banks_kernel(
 
         best_bc, best = {}, {}
 
-        def max_bc(s):
-            first = 1 if s < PACK else 0
-            for a in range(first, PASSES):
-                first_pass("b", s, a)
-            b_sb = sb("b_sb%d" % s, [P, HALF], F32)
-            nc.scalar.copy(b_sb[:], acc["b", s][:])
-            for a in range(first, PASSES):
+        c_sb = {}
+
+        def copy_c(s):
+            if s < 2:
+                c_sb[s] = shared.tile([P, HALF], F32, name="c_sb%d" % s, offset=4 * HALF * s)
+            else:
+                c_sb[s] = sb("c_sb%d" % s, [P, HALF], F32)
+            nc.scalar.copy(c_sb[s][:], acc["c", s][:])
+
+        def make_c(s):
+            for a in range(PASSES):
                 first_pass("c", s, a)
+            copy_c(s)
+
+        def max_bc(s):
+            for a in range(PASSES):
+                first_pass("b", s, a)
             best_bc[s] = sb("best_bc%d" % s, [P, HALF], F32)
-            nc.vector.tensor_tensor(best_bc[s][:], acc["c", s][:], b_sb[:], MAX)
+            nc.vector.tensor_tensor(best_bc[s][:], acc["b", s][:], c_sb[s][:], MAX)
 
         def max_abc(s):
             for a in range(PASSES):
@@ -231,36 +246,46 @@ def tile_list_fresh_passage_banks_kernel(
                     nc.scalar.activation(res[:, u, :], y[:, 0:width], IDENTITY, bias=bias[:, u : u + 1])
             nc.sync.dma_start(out[:, j0 : j0 + width].rearrange("(u p) j -> p u j", p=P), res[:])
 
-        for s in range(PACK):
-            for kind in "bc":
-                first_pass(kind, s, 0)
-        for s in range(PACK):
+        for s in range(2):
+            first_pass("c", s, 0)
+        for s in range(2):
+            first_pass("c", s, 1)
+            copy_c(s)
+        for s in range(2):
             max_bc(s)
-            if s % 2 == 1:
-                round_wa(1, s - 1, 2)
-                quantise_wa(1, s - 1, 2)
-        load_fresh(3)
-        bias = sb("bias", [P, N // P], F32)
-        with nc.allow_non_contiguous_dma("one bias value for each partition"):
-            nc.sync.dma_start(bias[:], b2.rearrange("(u p) -> p u", p=P))
+        round_wa(0, 0, 2, nc.scalar.copy)
+        quantise_wa(0, 0, 2)
+        for s in (2, 3):
+            make_c(s)
+            max_bc(s)
+        round_wa(1, 0, 2, nc.vector.tensor_copy)
+        quantise_wa(1, 0, 2)
+        make_c(4)
+        max_bc(4)
+        for a in range(PASSES):
+            round_wa(a, 2, 2, nc.scalar.copy)
         h_f32[0] = sb("h_first", [P, PACK, HALF], F32)
+        max_abc(0)
+        max_abc(1)
+        weigh(0, 0, HALF)
+        for a in range(PASSES):
+            quantise_wa(a, 2, 2)
+        max_abc(4)
+        make_c(5)
+        max_bc(5)
+        max_abc(5)
+        weigh(1, 0, HALF)
         w2_bf = sb("w2_bf", [P, N * PACK], BF16)
         w2_codes = sb("w2_codes", [P, N], U32)
         w2_plane = sb("w2_plane", [P, N], U8)
         interleave(nc.scalar.copy, w2_bf[:], w2_raw[:])
-        nc.vector.quantize_mx(out=w2_codes[:].bitcast(E4M3), scales=w2_plane[:], in_=w2_bf[:])
-        max_bc(4)
-        max_abc(0)
-        max_abc(1)
-        weigh(0, 0, HALF)
-        max_abc(4)
-        max_bc(5)
         max_abc(2)
         max_abc(3)
-        weigh(1, 0, HALF)
-        max_abc(5)
+        make_c(6)
         max_bc(6)
+        nc.vector.quantize_mx(out=w2_codes[:].bitcast(E4M3), scales=w2_plane[:], in_=w2_bf[:])
         weigh(2, 0, HALF)
+        make_c(7)
         max_bc(7)
         max_abc(6)
         max_abc(7)

@@ -23,7 +23,7 @@ PASSES = K // (P * PACK)
 HALF = 512
 UNITS = PACK * S // HALF
 CHUNKS = ((0, 256), (256, 256), (512, 256), (768, 128), (896, 128))
-BANKS = {"a": (2, 3, 6, 7, 1, 5, 0, 4), "b": (4, 5, 6, 7, 4, 3, 5, 7), "c": (0, 1, 0, 1, 0, 2, 1, 6)}
+BANKS = {"a": (2, 3, 6, 7, 0, 1, 4, 5), "b": (4, 5, 6, 7, 4, 5, 3, 1), "c": (0, 1, 0, 1, 0, 1, 2, 0)}
 LIVE = 96
 STAGE = 64
 
@@ -51,7 +51,7 @@ def tile_list_fresh_passage_banks_kernel(
 
         w_rows = sb("w_rows", [P, H], U8)
         for w, scales in enumerate((wc_scales, wb_scales)):
-            nc.sync.dma_start(
+            nc.scalar.dma_start(
                 w_rows[STAGE + w : P : 2, :].bitcast(I32), scales.rearrange("a q e -> q a e").bitcast(I32)
             )
         tab_plane = sb("tab_plane", [P, T], U8)
@@ -260,8 +260,9 @@ def tile_list_fresh_passage_banks_kernel(
             max_bc(s)
         round_wa(1, 0, 2, nc.vector.tensor_copy)
         quantise_wa(1, 0, 2)
-        make_c(4)
-        max_bc(4)
+        for s in (4, 5):
+            make_c(s)
+            max_bc(s)
         for a in range(PASSES):
             round_wa(a, 2, 2, nc.scalar.copy)
         h_f32[0] = sb("h_first", [P, PACK, HALF], F32)
@@ -271,8 +272,8 @@ def tile_list_fresh_passage_banks_kernel(
         for a in range(PASSES):
             quantise_wa(a, 2, 2)
         max_abc(4)
-        make_c(5)
-        max_bc(5)
+        make_c(6)
+        max_bc(6)
         max_abc(5)
         weigh(1, 0, HALF)
         w2_bf = sb("w2_bf", [P, N * PACK], BF16)
@@ -281,8 +282,6 @@ def tile_list_fresh_passage_banks_kernel(
         interleave(nc.scalar.copy, w2_bf[:], w2_raw[:])
         max_abc(2)
         max_abc(3)
-        make_c(6)
-        max_bc(6)
         nc.vector.quantize_mx(out=w2_codes[:].bitcast(E4M3), scales=w2_plane[:], in_=w2_bf[:])
         weigh(2, 0, HALF)
         make_c(7)

@@ -86,7 +86,7 @@ def tile_list_fresh_passage_banks_kernel(
 
         w_rows_dealt = sb("w_rows_dealt", [P, H], U8)
         deal(nc.vector.tensor_copy, w_rows_dealt[:], w_rows[:], "p t m")
-        for q in range(4):
+        for q in (0, 2, 1, 3):
             nc.sync.dma_start(
                 w_planes[32 * q : 32 * q + 4, :].bitcast(I32).rearrange("r (x e) -> r x e", x=2 * PASSES),
                 w_rows_dealt[STAGE + 16 * q : STAGE + 16 * q + 16, :].bitcast(I32),
@@ -94,7 +94,7 @@ def tile_list_fresh_passage_banks_kernel(
         load_tab(1)
         picked_plane = sb("picked_plane", [P, S], U8)
         nc.vector.tensor_copy(picked_plane[:], tab_plane[:].indirect(offsets[:]))
-        for q in range(4):
+        for q in (0, 2, 1, 3):
             nc.sync.dma_start(
                 v_planes[32 * q : 32 * q + 4, :].bitcast(I32).rearrange("r (a j) -> r a j", a=PASSES),
                 picked_plane[LIVE + 8 * q : LIVE + 8 * q + 8, :].bitcast(I32),

@@ -1,6 +1,7 @@
 from contextlib import ExitStack
 
 import concourse.mybir as mybir
+from concourse.masks import make_identity
 
 K, T, S, H, N = 1024, 2048, 1024, 512, 256
 FLOPS = 2 * K * H * S * 3 + 2 * H * N * S
@@ -16,6 +17,8 @@ E2M1 = mybir.dt.float4_e2m1fn_x4
 MAX = mybir.AluOpType.max
 MULT = mybir.AluOpType.mult
 IDENTITY = mybir.ActivationFunctionType.Identity
+COPY = mybir.ActivationFunctionType.Copy
+RELU = mybir.ActivationFunctionType.Relu
 
 P = 128
 PACK = 4
@@ -23,7 +26,8 @@ PASSES = K // (P * PACK)
 HALF = 512
 UNITS = PACK * S // HALF
 CHUNKS = ((0, 256), (256, 256), (512, 256), (768, 128), (896, 128))
-BANKS = {"a": (2, 3, 6, 7, 0, 1, 4, 5), "b": (4, 5, 6, 7, 4, 5, 3, 1), "c": (0, 1, 0, 1, 0, 1, 2, 0)}
+BANKS = {"a": (2, 3, 6, 7, 0, 1, 2, 5), "b": (4, 5, 6, 7, 4, 5, 3, 3), "c": (0, 1, 2, 3, 0, 1, 2, 2)}
+TURN_BANKS = {7: (4, 5, 4)}
 LIVE = 96
 STAGE = 64
 
@@ -99,8 +103,10 @@ def tile_list_fresh_passage_banks_kernel(
                 v_planes[32 * q : 32 * q + 4, :].bitcast(I32).rearrange("r (a j) -> r a j", a=PASSES),
                 picked_plane[LIVE + 8 * q : LIVE + 8 * q + 8, :].bitcast(I32),
             )
-        wb_raw = shared.tile([P, PASSES, H], I32, name="wb_raw", offset=0)
-        nc.sync.dma_start(wb_raw[:], wb_words.rearrange("a p e i -> p a (e i)").bitcast(I32))
+        wb_raw = {}
+        for a in range(PASSES):
+            wb_raw[a] = shared.tile([P, H], I32, name="wb_raw%d" % a, offset=4 * HALF * (PACK - 1 + a))
+            nc.sync.dma_start(wb_raw[a][:], wb_words[a].rearrange("p e i -> p (e i)").bitcast(I32))
         load_wa(0)
         load_wa(1)
         load_fresh(0)
@@ -114,48 +120,59 @@ def tile_list_fresh_passage_banks_kernel(
             nc.sync.dma_start(bias[:], b2.rearrange("(u p) -> p u", p=P))
         v_plane = [v_planes[:, a * S : (a + 1) * S] for a in range(PASSES)]
 
-        v_codes = [sb("v_codes%d" % a, [P, S], U32) for a in range(PASSES)]
+        v_codes = {(a, hf): sb("v_codes%d_%d" % (a, hf), [P, HALF], U32) for a, hf in ((0, 0), (0, 1), (1, 0))}
 
         def gather_codes(a, j0, width):
-            nc.vector.tensor_copy(v_codes[a][:, j0 : j0 + width], tab_w[a][:].bitcast(U32).indirect(picks(j0, width)))
-
-        wa_bf = [sb("wa_bf%d" % a, [P, H * PACK], BF16) for a in range(PASSES)]
-        wa_codes = [sb("wa_codes%d" % a, [P, H], U32) for a in range(PASSES)]
-        wa_plane = [sb("wa_plane%d" % a, [P, H], U8) for a in range(PASSES)]
-
-        def round_wa(a, t0, count, copy):
-            copy(
-                wa_bf[a][:].rearrange("p (t m k) -> p m k t", t=PACK, k=PACK)[:, :, :, t0 : t0 + count],
-                wa_raw[a][:].rearrange("p k (m t) -> p m k t", t=PACK)[:, :, :, t0 : t0 + count],
+            hf, c0 = divmod(j0, HALF)
+            nc.vector.tensor_copy(
+                v_codes[a, hf][:, c0 : c0 + width], tab_w[a][:].bitcast(U32).indirect(picks(j0, width))
             )
 
-        def quantise_wa(a, t0, count):
-            cols = slice(t0 * P, (t0 + count) * P)
+        wa_bf = {}
+        wa_codes = [sb("wa_codes%d" % pair, [P, PASSES, 2 * P], U32) for pair in range(2)]
+        wa_plane = [sb("wa_plane%d" % pair, [P, PASSES, 2 * P], U8) for pair in range(2)]
+
+        def round_wa(a, pair, copy):
+            if a == 0:
+                if pair == 0:
+                    wa_bf[pair] = sb("wa_bf0", [P, PASSES, 2 * H], BF16)
+                else:
+                    wa_bf[pair] = shared.tile([P, PASSES, 2 * H], BF16, name="wa_bf1", offset=0, align_bytes=64)
+            copy(
+                wa_bf[pair][:, a, :].rearrange("p (t m k) -> p m k t", t=2, k=PACK),
+                wa_raw[a][:].rearrange("p k (m t) -> p m k t", t=PACK)[:, :, :, 2 * pair : 2 * pair + 2],
+            )
+
+        def quantise_wa(pair, a0, count):
+            def flat(tile):
+                return tile[:, a0 : a0 + count, :].rearrange("p a c -> p (a c)")
+
             nc.vector.quantize_mx(
-                out=wa_codes[a][:, cols].bitcast(E4M3), scales=wa_plane[a][:, cols],
-                in_=wa_bf[a][:, t0 * H : (t0 + count) * H],
+                out=flat(wa_codes[pair]).bitcast(E4M3), scales=flat(wa_plane[pair]), in_=flat(wa_bf[pair])
             )
 
         wc_codes = [sb("wc_codes%d" % a, [P, H], U16) for a in range(PASSES)]
-        wb_codes = sb("wb_codes", [P, PASSES, H], U32)
+        wb_codes = [sb("wb_codes%d" % a, [P, H], U32) for a in range(PASSES)]
         for a in range(PASSES):
             deal(nc.scalar.copy, wc_codes[a][:], wc_raw[:, a, :].bitcast(U16), "p t m")
-        for a in range(PASSES):
-            gather_codes(a, 0, HALF)
-            gather_codes(a, HALF, HALF)
-        nc.scalar.copy(
-            wb_codes[:].rearrange("p a (t m) -> p a m t", t=PACK),
-            wb_raw[:].bitcast(U32).rearrange("p a (m t) -> p a m t", t=PACK),
-        )
+        gather_codes(0, 0, HALF // 2)
+        gather_codes(0, HALF // 2, HALF // 2)
+        gather_codes(0, HALF, HALF)
+        gather_codes(1, 0, HALF)
+        for a, copy in enumerate((nc.scalar.copy, nc.vector.tensor_copy)):
+            deal(copy, wb_codes[a][:], wb_raw[a][:].bitcast(U32), "p m t")
+        v_codes[1, 1] = shared.tile([P, HALF], U32, name="v_codes1_1", offset=4 * HALF * PACK, align_bytes=64)
+        gather_codes(1, HALF, HALF)
 
         def stationary(kind, a, t):
             cols = slice(t * P, (t + 1) * P)
             if kind == "a":
-                return wa_codes[a][:, cols].bitcast(E4M3), wa_plane[a][:, cols]
+                cols = slice(t % 2 * P, (t % 2 + 1) * P)
+                return wa_codes[t // 2][:, a, cols].bitcast(E4M3), wa_plane[t // 2][:, a, cols]
             w = 1 if kind == "b" else 0
             e0 = (2 * a + w) * H + t * P
             if kind == "b":
-                return wb_codes[:, a, cols].bitcast(E4M3), w_planes[:, e0 : e0 + P]
+                return wb_codes[a][:, cols].bitcast(E4M3), w_planes[:, e0 : e0 + P]
             return wc_codes[a][:, cols].bitcast(E2M1), w_planes[:, e0 : e0 + P]
 
         acc = {}
@@ -168,20 +185,23 @@ def tile_list_fresh_passage_banks_kernel(
             moving_scales = v_plane[a][:, hf * HALF : (hf + 1) * HALF]
             nc.tensor.matmul_mx(
                 out=acc[kind, s][:], lhsT=codes, lhsT_scale=scales,
-                rhs=v_codes[a][:, hf * HALF : (hf + 1) * HALF].bitcast(E4M3), rhs_scale=moving_scales,
+                rhs=v_codes[a, hf][:].bitcast(E4M3), rhs_scale=moving_scales,
                 start=(a == 0), stop=(a == PASSES - 1),
             )
 
-        best_bc, best = {}, {}
+        best_bc, best, late = {}, {}, {}
 
         c_sb = {}
+        c_first = shared.tile([P, PACK, HALF], F32, name="c_first", offset=0)
 
         def copy_c(s):
-            if s < 2:
-                c_sb[s] = shared.tile([P, HALF], F32, name="c_sb%d" % s, offset=4 * HALF * s)
+            if s < PACK:
+                c_sb[s] = c_first[:, s, :]
+            elif s < PACK + 2:
+                c_sb[s] = shared.tile([P, HALF], F32, name="c_sb%d" % s, offset=4 * HALF * (s - PACK))[:]
             else:
-                c_sb[s] = sb("c_sb%d" % s, [P, HALF], F32)
-            nc.scalar.copy(c_sb[s][:], acc["c", s][:])
+                c_sb[s] = sb("c_sb%d" % s, [P, HALF], F32)[:]
+            nc.scalar.copy(c_sb[s], acc["c", s][:])
 
         def make_c(s):
             for a in range(PASSES):
@@ -191,18 +211,70 @@ def tile_list_fresh_passage_banks_kernel(
         def max_bc(s):
             for a in range(PASSES):
                 first_pass("b", s, a)
-            best_bc[s] = sb("best_bc%d" % s, [P, HALF], F32)
-            nc.vector.tensor_tensor(best_bc[s][:], acc["b", s][:], c_sb[s][:], MAX)
+            best_bc[s] = late[0][:, 2, :] if s == 6 else sb("best_bc%d" % s, [P, HALF], F32)[:]
+            nc.vector.tensor_tensor(best_bc[s], acc["b", s][:], c_sb[s], MAX)
 
         def max_abc(s):
             for a in range(PASSES):
                 first_pass("a", s, a)
             width = CHUNKS[0][1] if s == PACK - 1 else HALF
             for c0 in range(0, HALF, width):
-                part = sb("best%d_%d" % (s, c0), [P, width], F32)
-                nc.vector.tensor_tensor(part[:], acc["a", s][:, c0 : c0 + width], best_bc[s][:, c0 : c0 + width], MAX)
+                if s == PACK:
+                    part = shared.tile([P, HALF], F32, name="best4", offset=0)[:]
+                elif s == PACK + 1:
+                    part = late[0][:, 1, :]
+                else:
+                    part = sb("best%d_%d" % (s, c0), [P, width], F32)[:]
+                nc.vector.tensor_tensor(part, acc["a", s][:, c0 : c0 + width], best_bc[s][:, c0 : c0 + width], MAX)
                 best[s, c0] = part
 
+        identity = sb("identity", [P, P], F32)
+        make_identity(nc, identity[:])
+
+        def turn(dst, sources):
+            for j in range(HALF // P):
+                cols = slice(j * P, (j + 1) * P)
+                for i, src in enumerate(sources):
+                    nc.tensor.matmul(
+                        dst[:, cols], src[:, cols], identity[:],
+                        start=(i == 0), stop=(i == len(sources) - 1), is_transpose=True,
+                    )
+
+        def copy_out_bc(s):
+            for a in range(PASSES):
+                first_pass("c", s, a)
+            minus_c[s] = sb("minus_c%d" % s, [P, HALF], F32)
+            nc.scalar.activation(minus_c[s][:], acc["c", s][:], COPY, scale=-1.0)
+            for a in range(PASSES):
+                first_pass("b", s, a)
+            b_sb[s] = sb("b_sb%d" % s, [P, HALF], F32)
+            nc.scalar.copy(b_sb[s][:], acc["b", s][:])
+
+        def lead_of_b(s):
+            gap = bank("gap%d" % s, TURN_BANKS[s][0])
+            turn(gap, (b_sb[s], minus_c[s]))
+            minus_ct = bank("minus_ct%d" % s, TURN_BANKS[s][1])
+            turn(minus_ct, (minus_c[s],))
+            lead[s] = sb("lead%d" % s, [P, HALF], F32)
+            nc.scalar.activation(lead[s][:], gap[:], RELU)
+            c_t[s] = sb("c_t%d" % s, [P, HALF], F32)
+            nc.scalar.activation(c_t[s][:], minus_ct[:], COPY, scale=-1.0)
+
+        def turn_back(s):
+            top_bc[s] = bank("top_bc%d" % s, TURN_BANKS[s][2])
+            turn(top_bc[s], (lead[s], c_t[s]))
+
+        def copy_out_a(s):
+            for a in range(PASSES):
+                first_pass("a", s, a)
+            a_sb[s] = sb("a_sb%d" % s, [P, HALF], F32)
+            nc.scalar.copy(a_sb[s][:], acc["a", s][:])
+
+        def max_off(s):
+            best[s, 0] = late[0][:, s - PACK, :]
+            nc.vector.tensor_tensor(best[s, 0], top_bc[s][:], a_sb[s][:], MAX)
+
+        minus_c, b_sb, lead, c_t, a_sb, top_bc = {}, {}, {}, {}, {}, {}
         h_f32 = {}
 
         def h_chunk(j0, width):
@@ -246,61 +318,65 @@ def tile_list_fresh_passage_banks_kernel(
                     nc.scalar.activation(res[:, u, :], y[:, 0:width], IDENTITY, bias=bias[:, u : u + 1])
             nc.sync.dma_start(out[:, j0 : j0 + width].rearrange("(u p) j -> p u j", p=P), res[:])
 
-        for s in range(2):
+        idle = bank("idle", BANKS["b"][PACK - 1])
+        for i in range(6):
+            codes, scales = stationary("c", 0, 0)
+            nc.tensor.matmul_mx(
+                out=idle[:, 0:256], lhsT=codes, lhsT_scale=scales,
+                rhs=v_codes[0, 0][:, 0:256].bitcast(E4M3), rhs_scale=w_planes[:, 0:256], start=True, stop=True,
+            )
+        for s in range(PACK):
             first_pass("c", s, 0)
-        for s in range(2):
+        for s in range(PACK):
             first_pass("c", s, 1)
             copy_c(s)
-        for s in range(2):
             max_bc(s)
-        round_wa(0, 0, 2, nc.scalar.copy)
-        quantise_wa(0, 0, 2)
-        for s in (2, 3):
-            make_c(s)
-            max_bc(s)
-        round_wa(1, 0, 2, nc.vector.tensor_copy)
-        quantise_wa(1, 0, 2)
+        for a in range(PASSES):
+            round_wa(a, 0, nc.vector.tensor_copy)
+            quantise_wa(0, a, 1)
         for s in (4, 5):
             make_c(s)
             max_bc(s)
         for a in range(PASSES):
-            round_wa(a, 2, 2, nc.scalar.copy)
+            round_wa(a, 1, nc.scalar.copy)
         h_f32[0] = sb("h_first", [P, PACK, HALF], F32)
         max_abc(0)
         max_abc(1)
+        quantise_wa(1, 0, PASSES)
         weigh(0, 0, HALF)
-        for a in range(PASSES):
-            quantise_wa(a, 2, 2)
-        max_abc(4)
-        make_c(6)
-        max_bc(6)
-        max_abc(5)
         weigh(1, 0, HALF)
         w2_bf = sb("w2_bf", [P, N * PACK], BF16)
         w2_codes = sb("w2_codes", [P, N], U32)
         w2_plane = sb("w2_plane", [P, N], U8)
-        interleave(nc.scalar.copy, w2_bf[:], w2_raw[:])
+        max_abc(4)
         max_abc(2)
         max_abc(3)
-        nc.vector.quantize_mx(out=w2_codes[:].bitcast(E4M3), scales=w2_plane[:], in_=w2_bf[:])
         weigh(2, 0, HALF)
-        make_c(7)
-        max_bc(7)
-        max_abc(6)
-        max_abc(7)
+        for step in (copy_out_bc, lead_of_b, turn_back, copy_out_a):
+            step(7)
+        interleave(nc.scalar.copy, w2_bf[:], w2_raw[:])
+        nc.vector.quantize_mx(out=w2_codes[:].bitcast(E4M3), scales=w2_plane[:], in_=w2_bf[:])
         for j0, width in CHUNKS[:2]:
             weigh(PACK - 1, j0, width)
             round_h(j0, width, nc.scalar.copy)
-        h_tags = ("best%d_0" % (PACK - 1), "h_first", "best%d_0" % (PACK - 1))
+        late[0] = sb("late", [P, PACK, HALF], F32, "best%d_0" % (PACK - 1))
+        max_abc(5)
+        make_c(6)
+        max_bc(6)
+        mix(CHUNKS[0][0], CHUNKS[0][1], (6, 7), False)
+        max_abc(6)
+        max_off(7)
+        mix(CHUNKS[1][0], CHUNKS[1][1], (0, 1), False)
+        h_tags = ("h_even", "a_sb7", "h_even")
         for c in range(2, len(CHUNKS)):
             j0, width = CHUNKS[c]
             h_f32[j0] = sb("h_f32_%d" % j0, [P, PACK, width], F32, h_tags[c - 2])
+            if c == 4:
+                mix(CHUNKS[2][0], CHUNKS[2][1], (3, 5), False)
             for t in range(PACK):
                 weigh(t, j0, width)
             if c < len(CHUNKS) - 1:
                 round_h(j0, width, nc.scalar.copy)
-            if c == 2:
-                mix(CHUNKS[0][0], CHUNKS[0][1], (0, 1), False)
-            mix(CHUNKS[c - 1][0], CHUNKS[c - 1][1], (2 * c - 2, 2 * c - 1), False)
+        mix(CHUNKS[3][0], CHUNKS[3][1], (2, 4), False)
         round_h(CHUNKS[-1][0], CHUNKS[-1][1], nc.vector.tensor_copy)
-        mix(CHUNKS[-1][0], CHUNKS[-1][1], (0, 1), True)
+        mix(CHUNKS[-1][0], CHUNKS[-1][1], (6, 7), True)

@@ -26,8 +26,9 @@ PASSES = K // (P * PACK)
 HALF = 512
 UNITS = PACK * S // HALF
 CHUNKS = ((0, 256), (256, 256), (512, 256), (768, 128), (896, 128))
-BANKS = {"a": (2, 3, 6, 7, 0, 1, 2, 5), "b": (4, 5, 6, 7, 4, 5, 3, 3), "c": (0, 1, 2, 3, 0, 1, 2, 2)}
-TURN_BANKS = {7: (4, 5, 4)}
+BANKS = {"a": (2, 3, 6, 7, 2, 3, 0, 4), "b": (4, 5, 6, 7, 4, 5, 2, 5), "c": (0, 1, 2, 3, 0, 1, 5, 3)}
+TURN_BANKS = {6: (0, 1, 1), 7: (4, 5, 5)}
+C_AT = {2: 0, 3: 4 * HALF * (PACK - 1), 4: 4 * HALF * (PACK - 1)}
 LIVE = 96
 STAGE = 64
 
@@ -189,16 +190,13 @@ def tile_list_fresh_passage_banks_kernel(
                 start=(a == 0), stop=(a == PASSES - 1),
             )
 
-        best_bc, best, late = {}, {}, {}
+        best_bc, best = {}, {}
 
         c_sb = {}
-        c_first = shared.tile([P, PACK, HALF], F32, name="c_first", offset=0)
 
         def copy_c(s):
-            if s < PACK:
-                c_sb[s] = c_first[:, s, :]
-            elif s < PACK + 2:
-                c_sb[s] = shared.tile([P, HALF], F32, name="c_sb%d" % s, offset=4 * HALF * (s - PACK))[:]
+            if s in C_AT:
+                c_sb[s] = shared.tile([P, HALF], F32, name="c_sb%d" % s, offset=C_AT[s])[:]
             else:
                 c_sb[s] = sb("c_sb%d" % s, [P, HALF], F32)[:]
             nc.scalar.copy(c_sb[s], acc["c", s][:])
@@ -211,22 +209,17 @@ def tile_list_fresh_passage_banks_kernel(
         def max_bc(s):
             for a in range(PASSES):
                 first_pass("b", s, a)
-            best_bc[s] = late[0][:, 2, :] if s == 6 else sb("best_bc%d" % s, [P, HALF], F32)[:]
+            best_bc[s] = sb("best_bc%d" % s, [P, HALF], F32)[:]
             nc.vector.tensor_tensor(best_bc[s], acc["b", s][:], c_sb[s], MAX)
 
         def max_abc(s):
             for a in range(PASSES):
                 first_pass("a", s, a)
-            width = CHUNKS[0][1] if s == PACK - 1 else HALF
-            for c0 in range(0, HALF, width):
-                if s == PACK:
-                    part = shared.tile([P, HALF], F32, name="best4", offset=0)[:]
-                elif s == PACK + 1:
-                    part = late[0][:, 1, :]
-                else:
-                    part = sb("best%d_%d" % (s, c0), [P, width], F32)[:]
-                nc.vector.tensor_tensor(part, acc["a", s][:, c0 : c0 + width], best_bc[s][:, c0 : c0 + width], MAX)
-                best[s, c0] = part
+            if s == PACK:
+                best[s, 0] = shared.tile([P, HALF], F32, name="best4", offset=0)[:]
+            else:
+                best[s, 0] = sb("best%d_0" % s, [P, HALF], F32, "best2_0" if s == PACK + 1 else "")[:]
+            nc.vector.tensor_tensor(best[s, 0], acc["a", s][:], best_bc[s], MAX)
 
         identity = sb("identity", [P, P], F32)
         make_identity(nc, identity[:])
@@ -271,7 +264,7 @@ def tile_list_fresh_passage_banks_kernel(
             nc.scalar.copy(a_sb[s][:], acc["a", s][:])
 
         def max_off(s):
-            best[s, 0] = late[0][:, s - PACK, :]
+            best[s, 0] = sb("best%d_0" % s, [P, HALF], F32)[:]
             nc.vector.tensor_tensor(best[s, 0], top_bc[s][:], a_sb[s][:], MAX)
 
         minus_c, b_sb, lead, c_t, a_sb, top_bc = {}, {}, {}, {}, {}, {}
@@ -285,7 +278,7 @@ def tile_list_fresh_passage_banks_kernel(
         def weigh(t, j0, width):
             hf, c0 = divmod(j0, HALF)
             s = hf * PACK + t
-            chosen = best[s, c0][:, 0:width] if s == PACK - 1 else best[s, 0][:, c0 : c0 + width]
+            chosen = best[s, 0][:, c0 : c0 + width]
             nc.vector.tensor_tensor(h_chunk(j0, width)[:, t, :], fresh[t][:].indirect(picks(j0, width)), chosen, MULT)
 
         def interleave(copy, dst, src):
@@ -348,35 +341,36 @@ def tile_list_fresh_passage_banks_kernel(
         w2_bf = sb("w2_bf", [P, N * PACK], BF16)
         w2_codes = sb("w2_codes", [P, N], U32)
         w2_plane = sb("w2_plane", [P, N], U8)
+        for s in (6, 7):
+            copy_out_bc(s)
         max_abc(4)
         max_abc(2)
         max_abc(3)
         weigh(2, 0, HALF)
-        for step in (copy_out_bc, lead_of_b, turn_back, copy_out_a):
-            step(7)
+        for step in (lead_of_b, copy_out_a, turn_back):
+            for s in (6, 7):
+                step(s)
         interleave(nc.scalar.copy, w2_bf[:], w2_raw[:])
         nc.vector.quantize_mx(out=w2_codes[:].bitcast(E4M3), scales=w2_plane[:], in_=w2_bf[:])
+        weigh(PACK - 1, 0, HALF)
         for j0, width in CHUNKS[:2]:
-            weigh(PACK - 1, j0, width)
             round_h(j0, width, nc.scalar.copy)
-        late[0] = sb("late", [P, PACK, HALF], F32, "best%d_0" % (PACK - 1))
         max_abc(5)
-        make_c(6)
-        max_bc(6)
-        mix(CHUNKS[0][0], CHUNKS[0][1], (6, 7), False)
-        max_abc(6)
-        max_off(7)
-        mix(CHUNKS[1][0], CHUNKS[1][1], (0, 1), False)
         h_tags = ("h_even", "a_sb7", "h_even")
         for c in range(2, len(CHUNKS)):
             j0, width = CHUNKS[c]
             h_f32[j0] = sb("h_f32_%d" % j0, [P, PACK, width], F32, h_tags[c - 2])
             if c == 4:
-                mix(CHUNKS[2][0], CHUNKS[2][1], (3, 5), False)
+                mix(CHUNKS[1][0], CHUNKS[1][1], (2, 0), False)
+                mix(CHUNKS[2][0], CHUNKS[2][1], (3, 4), False)
             for t in range(PACK):
+                if c == 2 and t == 2:
+                    max_off(6)
+                    max_off(7)
+                    mix(CHUNKS[0][0], CHUNKS[0][1], (6, 7), False)
                 weigh(t, j0, width)
             if c < len(CHUNKS) - 1:
                 round_h(j0, width, nc.scalar.copy)
-        mix(CHUNKS[3][0], CHUNKS[3][1], (2, 4), False)
+        mix(CHUNKS[3][0], CHUNKS[3][1], (1, 5), False)
         round_h(CHUNKS[-1][0], CHUNKS[-1][1], nc.vector.tensor_copy)
         mix(CHUNKS[-1][0], CHUNKS[-1][1], (6, 7), True)

@@ -29,6 +29,7 @@ CHUNKS = ((0, 256), (256, 256), (512, 256), (768, 128), (896, 128))
 BANKS = {"a": (2, 3, 6, 7, 2, 3, 0, 4), "b": (4, 5, 6, 7, 4, 5, 2, 5), "c": (0, 1, 2, 3, 0, 1, 5, 3)}
 TURN_BANKS = {6: (0, 1, 1), 7: (4, 5, 5)}
 C_AT = {2: 0, 3: 4 * HALF * (PACK - 1), 4: 4 * HALF * (PACK - 1)}
+QUARTER = HALF // 2
 LIVE = 96
 STAGE = 64
 
@@ -156,8 +157,7 @@ def tile_list_fresh_passage_banks_kernel(
         wb_codes = [sb("wb_codes%d" % a, [P, H], U32) for a in range(PASSES)]
         for a in range(PASSES):
             deal(nc.scalar.copy, wc_codes[a][:], wc_raw[:, a, :].bitcast(U16), "p t m")
-        gather_codes(0, 0, HALF // 2)
-        gather_codes(0, HALF // 2, HALF // 2)
+        gather_codes(0, 0, HALF)
         gather_codes(0, HALF, HALF)
         gather_codes(1, 0, HALF)
         for a, copy in enumerate((nc.scalar.copy, nc.vector.tensor_copy)):
@@ -213,13 +213,17 @@ def tile_list_fresh_passage_banks_kernel(
             nc.vector.tensor_tensor(best_bc[s], acc["b", s][:], c_sb[s], MAX)
 
         def max_abc(s):
-            for a in range(PASSES):
-                first_pass("a", s, a)
-            if s == PACK:
-                best[s, 0] = shared.tile([P, HALF], F32, name="best4", offset=0)[:]
-            else:
-                best[s, 0] = sb("best%d_0" % s, [P, HALF], F32, "best2_0" if s == PACK + 1 else "")[:]
-            nc.vector.tensor_tensor(best[s, 0], acc["a", s][:], best_bc[s], MAX)
+            if ("a", s) not in acc:
+                for a in range(PASSES):
+                    first_pass("a", s, a)
+            width = CHUNKS[0][1] if s == PACK - 1 else HALF
+            for c0 in range(0, HALF, width):
+                if s == PACK:
+                    best[s, c0] = shared.tile([P, HALF], F32, name="best4", offset=0)[:]
+                else:
+                    best[s, c0] = sb("best%d_%d" % (s, c0), [P, width], F32, "best3_0" if s == PACK + 1 else "")[:]
+                cols = slice(c0, c0 + width)
+                nc.vector.tensor_tensor(best[s, c0], acc["a", s][:, cols], best_bc[s][:, cols], MAX)
 
         identity = sb("identity", [P, P], F32)
         make_identity(nc, identity[:])
@@ -253,21 +257,34 @@ def tile_list_fresh_passage_banks_kernel(
             c_t[s] = sb("c_t%d" % s, [P, HALF], F32)
             nc.scalar.activation(c_t[s][:], minus_ct[:], COPY, scale=-1.0)
 
-        def turn_back(s):
-            top_bc[s] = bank("top_bc%d" % s, TURN_BANKS[s][2])
-            turn(top_bc[s], (lead[s], c_t[s]))
+        def turn_back(part):
+            top_bc[part] = bank("top_bc%d" % part, TURN_BANKS[6 + part][2])
+            for i, s in enumerate((6, 7)):
+                for j in range(QUARTER // P):
+                    src = slice(part * QUARTER + j * P, part * QUARTER + (j + 1) * P)
+                    dst = slice(i * QUARTER + j * P, i * QUARTER + (j + 1) * P)
+                    for n, tile in enumerate((lead[s], c_t[s])):
+                        nc.tensor.matmul(
+                            top_bc[part][:, dst], tile[:, src], identity[:],
+                            start=(n == 0), stop=(n == 1), is_transpose=True,
+                        )
 
         def copy_out_a(s):
             for a in range(PASSES):
                 first_pass("a", s, a)
-            a_sb[s] = sb("a_sb%d" % s, [P, HALF], F32)
-            nc.scalar.copy(a_sb[s][:], acc["a", s][:])
+            nc.scalar.copy(a_late[:, :, s - 6, :], acc["a", s][:].rearrange("p (part c) -> p part c", part=2))
 
-        def max_off(s):
-            best[s, 0] = sb("best%d_0" % s, [P, HALF], F32)[:]
-            nc.vector.tensor_tensor(best[s, 0], top_bc[s][:], a_sb[s][:], MAX)
+        def max_off(part):
+            both = sb("best_late%d" % part, [P, 2, QUARTER], F32)
+            nc.vector.tensor_tensor(
+                both[:].rearrange("p s c -> p (s c)"), top_bc[part][:],
+                a_late[:, part, :, :].rearrange("p s c -> p (s c)"), MAX,
+            )
+            for i, s in enumerate((6, 7)):
+                best[s, part * QUARTER] = both[:, i, :]
 
-        minus_c, b_sb, lead, c_t, a_sb, top_bc = {}, {}, {}, {}, {}, {}
+        minus_c, b_sb, lead, c_t, top_bc = {}, {}, {}, {}, {}
+        a_late = sb("a_late", [P, 2, 2, QUARTER], F32)
         h_f32 = {}
 
         def h_chunk(j0, width):
@@ -278,7 +295,8 @@ def tile_list_fresh_passage_banks_kernel(
         def weigh(t, j0, width):
             hf, c0 = divmod(j0, HALF)
             s = hf * PACK + t
-            chosen = best[s, 0][:, c0 : c0 + width]
+            first = c0 // QUARTER * QUARTER if s in (3, 6, 7) else 0
+            chosen = best[s, first][:, c0 - first : c0 - first + width]
             nc.vector.tensor_tensor(h_chunk(j0, width)[:, t, :], fresh[t][:].indirect(picks(j0, width)), chosen, MULT)
 
         def interleave(copy, dst, src):
@@ -293,30 +311,41 @@ def tile_list_fresh_passage_banks_kernel(
             h_bf[j0] = sb("h_bf%d" % j0, [P, width * PACK], BF16)
             interleave(copy, h_bf[j0][:], h_chunk(j0, width))
 
-        def mix(j0, width, banks, last):
+        mixed = {}
+
+        def mix(j0, width, banks):
             h_codes = sb("h_codes%d" % j0, [P, width], U32)
             h_plane = sb("h_plane%d" % j0, [P, width], U8)
             nc.vector.quantize_mx(out=h_codes[:].bitcast(E4M3), scales=h_plane[:], in_=h_bf[j0][:])
-            res = sb("res%d" % j0, [P, N // P, width], F32)
             for u in range(N // P):
-                y = bank("y%d_%d" % (j0, u), banks[u])
+                mixed[j0, u] = bank("y%d_%d" % (j0, u), banks[u])
                 cols = slice(u * P, (u + 1) * P)
                 nc.tensor.matmul_mx(
-                    out=y[:, 0:width], lhsT=w2_codes[:, cols].bitcast(E4M3), lhsT_scale=w2_plane[:, cols],
+                    out=mixed[j0, u][:, 0:width], lhsT=w2_codes[:, cols].bitcast(E4M3), lhsT_scale=w2_plane[:, cols],
                     rhs=h_codes[:].bitcast(E4M3), rhs_scale=h_plane[:], start=True, stop=True,
                 )
+
+        def finish(j0, width, last):
+            res = sb("res%d" % j0, [P, N // P, width], F32)
+            for u in range(N // P):
+                y = mixed[j0, u][:, 0:width]
                 if last and u == 1:
-                    nc.vector.tensor_scalar_add(res[:, u, :], y[:, 0:width], bias[:, u : u + 1])
+                    nc.vector.tensor_scalar_add(res[:, u, :], y, bias[:, u : u + 1])
                 else:
-                    nc.scalar.activation(res[:, u, :], y[:, 0:width], IDENTITY, bias=bias[:, u : u + 1])
+                    nc.scalar.activation(res[:, u, :], y, IDENTITY, bias=bias[:, u : u + 1])
             nc.sync.dma_start(out[:, j0 : j0 + width].rearrange("(u p) j -> p u j", p=P), res[:])
 
         idle = bank("idle", BANKS["b"][PACK - 1])
-        for i in range(6):
+        for i in range(3):
+            nc.tensor.matmul_mx(
+                out=idle[:], lhsT=tab_w[0][:, 0:P].bitcast(E4M3), lhsT_scale=tab_plane[:, 0:P],
+                rhs=wc_raw[:, 0, :].bitcast(E2M1), rhs_scale=tab_plane[:, 0:HALF], start=True, stop=True,
+            )
+        for i in range(2):
             codes, scales = stationary("c", 0, 0)
             nc.tensor.matmul_mx(
-                out=idle[:, 0:256], lhsT=codes, lhsT_scale=scales,
-                rhs=v_codes[0, 0][:, 0:256].bitcast(E4M3), rhs_scale=w_planes[:, 0:256], start=True, stop=True,
+                out=idle[:], lhsT=codes, lhsT_scale=scales,
+                rhs=v_codes[0, 0][:].bitcast(E4M3), rhs_scale=w_planes[:, 0:HALF], start=True, stop=True,
             )
         for s in range(PACK):
             first_pass("c", s, 0)
@@ -347,30 +376,38 @@ def tile_list_fresh_passage_banks_kernel(
         max_abc(2)
         max_abc(3)
         weigh(2, 0, HALF)
-        for step in (lead_of_b, copy_out_a, turn_back):
+        for step in (lead_of_b, copy_out_a):
             for s in (6, 7):
                 step(s)
+        for a in range(PASSES):
+            first_pass("a", 5, a)
+        for part in range(2):
+            turn_back(part)
         interleave(nc.scalar.copy, w2_bf[:], w2_raw[:])
         nc.vector.quantize_mx(out=w2_codes[:].bitcast(E4M3), scales=w2_plane[:], in_=w2_bf[:])
-        weigh(PACK - 1, 0, HALF)
         for j0, width in CHUNKS[:2]:
+            weigh(PACK - 1, j0, width)
             round_h(j0, width, nc.scalar.copy)
         max_abc(5)
-        h_tags = ("h_even", "a_sb7", "h_even")
+        h_tags = ("h_even", "h_odd", "h_even")
         for c in range(2, len(CHUNKS)):
             j0, width = CHUNKS[c]
             h_f32[j0] = sb("h_f32_%d" % j0, [P, PACK, width], F32, h_tags[c - 2])
             if c == 4:
-                mix(CHUNKS[1][0], CHUNKS[1][1], (2, 0), False)
-                mix(CHUNKS[2][0], CHUNKS[2][1], (3, 4), False)
+                mix(*CHUNKS[1], (2, 0))
+                mix(*CHUNKS[2], (3, 4))
+                for done in CHUNKS[:3]:
+                    finish(*done, False)
             for t in range(PACK):
                 if c == 2 and t == 2:
-                    max_off(6)
-                    max_off(7)
-                    mix(CHUNKS[0][0], CHUNKS[0][1], (6, 7), False)
+                    mix(*CHUNKS[0], (6, 7))
+                if c in (2, 3) and t == 2:
+                    max_off(c - 2)
                 weigh(t, j0, width)
             if c < len(CHUNKS) - 1:
                 round_h(j0, width, nc.scalar.copy)
-        mix(CHUNKS[3][0], CHUNKS[3][1], (1, 5), False)
+        mix(*CHUNKS[3], (1, 5))
+        finish(*CHUNKS[3], False)
         round_h(CHUNKS[-1][0], CHUNKS[-1][1], nc.vector.tensor_copy)
-        mix(CHUNKS[-1][0], CHUNKS[-1][1], (6, 7), True)
+        mix(*CHUNKS[-1], (6, 7))
+        finish(*CHUNKS[-1], True)

@@ -16,6 +16,7 @@ E4M3 = mybir.dt.float8_e4m3fn_x4
 E2M1 = mybir.dt.float4_e2m1fn_x4
 MAX = mybir.AluOpType.max
 MULT = mybir.AluOpType.mult
+ADD = mybir.AluOpType.add
 IDENTITY = mybir.ActivationFunctionType.Identity
 COPY = mybir.ActivationFunctionType.Copy
 RELU = mybir.ActivationFunctionType.Relu
@@ -26,9 +27,10 @@ PASSES = K // (P * PACK)
 HALF = 512
 UNITS = PACK * S // HALF
 CHUNKS = ((0, 256), (256, 256), (512, 256), (768, 128), (896, 128))
-BANKS = {"a": (2, 3, 6, 7, 2, 3, 0, 4), "b": (4, 5, 6, 7, 4, 5, 2, 5), "c": (0, 1, 2, 3, 0, 1, 5, 3)}
-TURN_BANKS = {6: (0, 1, 1), 7: (4, 5, 5)}
+BANKS = {"a": (2, 3, 6, 7, 2, 3, 4, 0), "b": (4, 5, 6, 7, 0, 1, 2, 1), "c": (0, 1, 2, 3, 4, 5, 1, 3)}
+TURN_BANKS = {6: (4, 5, 5), 7: (0, 1, 1)}
 C_AT = {2: 0, 3: 4 * HALF * (PACK - 1), 4: 4 * HALF * (PACK - 1)}
+BC_AT = 4 * HALF * (PACK + 1)
 QUARTER = HALF // 2
 LIVE = 96
 STAGE = 64
@@ -130,28 +132,18 @@ def tile_list_fresh_passage_banks_kernel(
                 v_codes[a, hf][:, c0 : c0 + width], tab_w[a][:].bitcast(U32).indirect(picks(j0, width))
             )
 
-        wa_bf = {}
         wa_codes = [sb("wa_codes%d" % pair, [P, PASSES, 2 * P], U32) for pair in range(2)]
         wa_plane = [sb("wa_plane%d" % pair, [P, PASSES, 2 * P], U8) for pair in range(2)]
 
-        def round_wa(a, pair, copy):
-            if a == 0:
-                if pair == 0:
-                    wa_bf[pair] = sb("wa_bf0", [P, PASSES, 2 * H], BF16)
-                else:
-                    wa_bf[pair] = shared.tile([P, PASSES, 2 * H], BF16, name="wa_bf1", offset=0, align_bytes=64)
-            copy(
-                wa_bf[pair][:, a, :].rearrange("p (t m k) -> p m k t", t=2, k=PACK),
-                wa_raw[a][:].rearrange("p k (m t) -> p m k t", t=PACK)[:, :, :, 2 * pair : 2 * pair + 2],
-            )
+        def wa_views(rounded, a, pair, order):
+            raw = wa_raw[a][:].rearrange("p k (m u t) -> p u k m t", u=2, t=2)[:, pair]
+            return rounded.rearrange("p (t m k) -> " + order, t=2, k=PACK), raw.rearrange("p k m t -> " + order)
 
-        def quantise_wa(pair, a0, count):
+        def quantise_wa(pair, a0, count, rounded):
             def flat(tile):
                 return tile[:, a0 : a0 + count, :].rearrange("p a c -> p (a c)")
 
-            nc.vector.quantize_mx(
-                out=flat(wa_codes[pair]).bitcast(E4M3), scales=flat(wa_plane[pair]), in_=flat(wa_bf[pair])
-            )
+            nc.vector.quantize_mx(out=flat(wa_codes[pair]).bitcast(E4M3), scales=flat(wa_plane[pair]), in_=rounded)
 
         wc_codes = [sb("wc_codes%d" % a, [P, H], U16) for a in range(PASSES)]
         wb_codes = [sb("wb_codes%d" % a, [P, H], U32) for a in range(PASSES)]
@@ -209,7 +201,11 @@ def tile_list_fresh_passage_banks_kernel(
         def max_bc(s):
             for a in range(PASSES):
                 first_pass("b", s, a)
-            best_bc[s] = sb("best_bc%d" % s, [P, HALF], F32)[:]
+            if s < PACK:
+                best_bc[s] = sb("best_bc%d" % s, [P, HALF], F32)[:]
+            else:
+                at = BC_AT + 4 * HALF * (s - PACK)
+                best_bc[s] = shared.tile([P, HALF], F32, name="best_bc%d" % s, offset=at)[:]
             nc.vector.tensor_tensor(best_bc[s], acc["b", s][:], c_sb[s], MAX)
 
         def max_abc(s):
@@ -353,21 +349,25 @@ def tile_list_fresh_passage_banks_kernel(
             first_pass("c", s, 1)
             copy_c(s)
             max_bc(s)
-        for a in range(PASSES):
-            round_wa(a, 0, nc.vector.tensor_copy)
-            quantise_wa(0, a, 1)
+        early0 = sb("wa_early0", [P, 2 * H], BF16)
+        nc.gpsimd.tensor_scalar(*wa_views(early0[:], 0, 0, "p m t k"), 1.0, 0.0, MULT, ADD)
+        quantise_wa(0, 0, 1, early0[:])
+        early1 = shared.tile([P, 2 * H], BF16, name="wa_early1", offset=BC_AT + 2 * HALF, align_bytes=64)
+        nc.vector.tensor_copy(*wa_views(early1[:], 1, 0, "p m k t"))
+        quantise_wa(0, 1, 1, early1[:])
         for s in (4, 5):
             make_c(s)
             max_bc(s)
+        late = shared.tile([P, PASSES, 2 * H], BF16, name="wa_late", offset=0, align_bytes=64)
         for a in range(PASSES):
-            round_wa(a, 1, nc.scalar.copy)
+            nc.scalar.copy(*wa_views(late[:, a, :], a, 1, "p m k t"))
         h_f32[0] = sb("h_first", [P, PACK, HALF], F32)
         max_abc(0)
         max_abc(1)
-        quantise_wa(1, 0, PASSES)
+        quantise_wa(1, 0, PASSES, late[:].rearrange("p a c -> p (a c)"))
         weigh(0, 0, HALF)
         weigh(1, 0, HALF)
-        w2_bf = sb("w2_bf", [P, N * PACK], BF16)
+        w2_bf = sb("w2_bf", [P, N * PACK], BF16, "best1_0")
         w2_codes = sb("w2_codes", [P, N], U32)
         w2_plane = sb("w2_plane", [P, N], U8)
         for s in (6, 7):
@@ -383,7 +383,9 @@ def tile_list_fresh_passage_banks_kernel(
             first_pass("a", 5, a)
         for part in range(2):
             turn_back(part)
-        interleave(nc.scalar.copy, w2_bf[:], w2_raw[:])
+        nc.gpsimd.tensor_scalar(
+            w2_bf[:].rearrange("p (n t) -> p n t", t=PACK), w2_raw[:].rearrange("p t n -> p n t"), 1.0, 0.0, MULT, ADD
+        )
         nc.vector.quantize_mx(out=w2_codes[:].bitcast(E4M3), scales=w2_plane[:], in_=w2_bf[:])
         for j0, width in CHUNKS[:2]:
             weigh(PACK - 1, j0, width)
@@ -394,8 +396,8 @@ def tile_list_fresh_passage_banks_kernel(
             j0, width = CHUNKS[c]
             h_f32[j0] = sb("h_f32_%d" % j0, [P, PACK, width], F32, h_tags[c - 2])
             if c == 4:
-                mix(*CHUNKS[1], (2, 0))
-                mix(*CHUNKS[2], (3, 4))
+                mix(*CHUNKS[1], (2, 4))
+                mix(*CHUNKS[2], (3, 0))
                 for done in CHUNKS[:3]:
                     finish(*done, False)
             for t in range(PACK):
@@ -406,7 +408,7 @@ def tile_list_fresh_passage_banks_kernel(
                 weigh(t, j0, width)
             if c < len(CHUNKS) - 1:
                 round_h(j0, width, nc.scalar.copy)
-        mix(*CHUNKS[3], (1, 5))
+        mix(*CHUNKS[3], (5, 1))
         finish(*CHUNKS[3], False)
         round_h(CHUNKS[-1][0], CHUNKS[-1][1], nc.vector.tensor_copy)
         mix(*CHUNKS[-1], (6, 7))

@@ -27,8 +27,8 @@ PASSES = K // (P * PACK)
 HALF = 512
 UNITS = PACK * S // HALF
 CHUNKS = ((0, 256), (256, 256), (512, 256), (768, 128), (896, 128))
-BANKS = {"a": (2, 3, 6, 7, 2, 3, 4, 0), "b": (4, 5, 6, 7, 0, 1, 2, 1), "c": (0, 1, 2, 3, 4, 5, 1, 3)}
-TURN_BANKS = {6: (4, 5, 5), 7: (0, 1, 1)}
+BANKS = {"a": (2, 3, 6, 7, 2, 3), "b": (4, 5, 6, 7, 0, 1, 2, 1), "c": (0, 1, 2, 3, 4, 5, 1, 3)}
+TURN_BANKS = ((4, 5), (0, 1))
 C_AT = {2: 0, 3: 4 * HALF * (PACK - 1), 4: 4 * HALF * (PACK - 1)}
 BC_AT = 4 * HALF * (PACK + 1)
 QUARTER = HALF // 2
@@ -226,12 +226,18 @@ def tile_list_fresh_passage_banks_kernel(
 
         def turn(dst, sources):
             for j in range(HALF // P):
-                cols = slice(j * P, (j + 1) * P)
                 for i, src in enumerate(sources):
                     nc.tensor.matmul(
-                        dst[:, cols], src[:, cols], identity[:],
+                        dst[:, j * P : (j + 1) * P], src(j), identity[:],
                         start=(i == 0), stop=(i == len(sources) - 1), is_transpose=True,
                     )
+
+        def block_of(tiles, part):
+            def block(j):
+                i, c0 = divmod(j * P, QUARTER)
+                return tiles[6 + i][:, part * QUARTER + c0 : part * QUARTER + c0 + P]
+
+            return block
 
         def copy_out_bc(s):
             for a in range(PASSES):
@@ -243,44 +249,41 @@ def tile_list_fresh_passage_banks_kernel(
             b_sb[s] = sb("b_sb%d" % s, [P, HALF], F32)
             nc.scalar.copy(b_sb[s][:], acc["b", s][:])
 
-        def lead_of_b(s):
-            gap = bank("gap%d" % s, TURN_BANKS[s][0])
-            turn(gap, (b_sb[s], minus_c[s]))
-            minus_ct = bank("minus_ct%d" % s, TURN_BANKS[s][1])
-            turn(minus_ct, (minus_c[s],))
-            lead[s] = sb("lead%d" % s, [P, HALF], F32)
-            nc.scalar.activation(lead[s][:], gap[:], RELU)
-            c_t[s] = sb("c_t%d" % s, [P, HALF], F32)
-            nc.scalar.activation(c_t[s][:], minus_ct[:], COPY, scale=-1.0)
+        def lead_of_b(part):
+            gap = bank("gap%d" % part, TURN_BANKS[part][0])
+            turn(gap, (block_of(b_sb, part), block_of(minus_c, part)))
+            minus_ct = bank("minus_ct%d" % part, TURN_BANKS[part][1])
+            turn(minus_ct, (block_of(minus_c, part),))
+            lead[part] = sb("lead%d" % part, [P, HALF], F32)
+            nc.scalar.activation(lead[part][:], gap[:], RELU)
+            c_t[part] = sb("c_t%d" % part, [P, HALF], F32)
+            nc.scalar.activation(c_t[part][:], minus_ct[:], COPY, scale=-1.0)
 
         def turn_back(part):
-            top_bc[part] = bank("top_bc%d" % part, TURN_BANKS[6 + part][2])
-            for i, s in enumerate((6, 7)):
-                for j in range(QUARTER // P):
-                    src = slice(part * QUARTER + j * P, part * QUARTER + (j + 1) * P)
-                    dst = slice(i * QUARTER + j * P, i * QUARTER + (j + 1) * P)
-                    for n, tile in enumerate((lead[s], c_t[s])):
-                        nc.tensor.matmul(
-                            top_bc[part][:, dst], tile[:, src], identity[:],
-                            start=(n == 0), stop=(n == 1), is_transpose=True,
-                        )
+            top_bc[part] = bank("top_bc%d" % part, TURN_BANKS[part][1])
+            turn(top_bc[part], [lambda j, tile=tile: tile[:, j * P : (j + 1) * P] for tile in (lead[part], c_t[part])])
 
-        def copy_out_a(s):
-            for a in range(PASSES):
-                first_pass("a", s, a)
-            nc.scalar.copy(a_late[:, :, s - 6, :], acc["a", s][:].rearrange("p (part c) -> p part c", part=2))
+        def copy_out_a(part):
+            late_a = bank("late_a%d" % part, TURN_BANKS[part][0])
+            for i in range(2):
+                for a in range(PASSES):
+                    codes, scales = stationary("a", a, 2 + i)
+                    j0 = HALF + part * QUARTER
+                    nc.tensor.matmul_mx(
+                        out=late_a[:, i * QUARTER : (i + 1) * QUARTER], lhsT=codes, lhsT_scale=scales,
+                        rhs=v_codes[a, 1][:, part * QUARTER : (part + 1) * QUARTER].bitcast(E4M3),
+                        rhs_scale=v_plane[a][:, j0 : j0 + QUARTER], start=(a == 0), stop=(a == PASSES - 1),
+                    )
+            a_sb[part] = sb("a_sb%d" % part, [P, HALF], F32)
+            nc.scalar.copy(a_sb[part][:], late_a[:])
 
         def max_off(part):
-            both = sb("best_late%d" % part, [P, 2, QUARTER], F32)
-            nc.vector.tensor_tensor(
-                both[:].rearrange("p s c -> p (s c)"), top_bc[part][:],
-                a_late[:, part, :, :].rearrange("p s c -> p (s c)"), MAX,
-            )
+            both = sb("best_late%d" % part, [P, HALF], F32)
+            nc.vector.tensor_tensor(both[:], top_bc[part][:], a_sb[part][:], MAX)
             for i, s in enumerate((6, 7)):
-                best[s, part * QUARTER] = both[:, i, :]
+                best[s, part * QUARTER] = both[:, i * QUARTER : (i + 1) * QUARTER]
 
-        minus_c, b_sb, lead, c_t, top_bc = {}, {}, {}, {}, {}
-        a_late = sb("a_late", [P, 2, 2, QUARTER], F32)
+        minus_c, b_sb, lead, c_t, top_bc, a_sb = {}, {}, {}, {}, {}, {}
         h_f32 = {}
 
         def h_chunk(j0, width):
@@ -376,13 +379,14 @@ def tile_list_fresh_passage_banks_kernel(
         max_abc(2)
         max_abc(3)
         weigh(2, 0, HALF)
-        for step in (lead_of_b, copy_out_a):
-            for s in (6, 7):
-                step(s)
+        for part in range(2):
+            lead_of_b(part)
+        copy_out_a(0)
         for a in range(PASSES):
             first_pass("a", 5, a)
-        for part in range(2):
-            turn_back(part)
+        turn_back(0)
+        copy_out_a(1)
+        turn_back(1)
         nc.gpsimd.tensor_scalar(
             w2_bf[:].rearrange("p (n t) -> p n t", t=PACK), w2_raw[:].rearrange("p t n -> p n t"), 1.0, 0.0, MULT, ADD
         )
@@ -396,15 +400,17 @@ def tile_list_fresh_passage_banks_kernel(
             j0, width = CHUNKS[c]
             h_f32[j0] = sb("h_f32_%d" % j0, [P, PACK, width], F32, h_tags[c - 2])
             if c == 4:
-                mix(*CHUNKS[1], (2, 4))
                 mix(*CHUNKS[2], (3, 0))
-                for done in CHUNKS[:3]:
-                    finish(*done, False)
+                finish(*CHUNKS[2], False)
             for t in range(PACK):
                 if c == 2 and t == 2:
                     mix(*CHUNKS[0], (6, 7))
+                    finish(*CHUNKS[0], False)
                 if c in (2, 3) and t == 2:
                     max_off(c - 2)
+                if c == 3 and t == 2:
+                    mix(*CHUNKS[1], (2, 4))
+                    finish(*CHUNKS[1], False)
                 weigh(t, j0, width)
             if c < len(CHUNKS) - 1:
                 round_h(j0, width, nc.scalar.copy)

@@ -353,7 +353,7 @@ def tile_list_fresh_passage_banks_kernel(
             copy_c(s)
             max_bc(s)
         early0 = sb("wa_early0", [P, 2 * H], BF16)
-        nc.gpsimd.tensor_scalar(*wa_views(early0[:], 0, 0, "p m t k"), 1.0, 0.0, MULT, ADD)
+        nc.vector.tensor_copy(*wa_views(early0[:], 0, 0, "p m k t"))
         quantise_wa(0, 0, 1, early0[:])
         early1 = shared.tile([P, 2 * H], BF16, name="wa_early1", offset=BC_AT + 2 * HALF, align_bytes=64)
         nc.vector.tensor_copy(*wa_views(early1[:], 1, 0, "p m k t"))

@@ -46,7 +46,7 @@ def tile_list_fresh_passage_banks_kernel(
         psum = ctx.enter_context(tc.psum_pool(name="psum", bufs=1))
 
         def sb(name, shape, dtype, tag=""):
-            return keep.tile(shape, dtype, name=name, tag=tag or name, align_bytes=64)
+            return keep.tile(shape, dtype, name=name, tag=tag or name, align_bytes=256)
 
         def bank(name, i):
             return psum.tile([P, HALF], F32, name=name, offset=2048 * i)
@@ -154,7 +154,7 @@ def tile_list_fresh_passage_banks_kernel(
         gather_codes(1, 0, HALF)
         for a, copy in enumerate((nc.scalar.copy, nc.vector.tensor_copy)):
             deal(copy, wb_codes[a][:], wb_raw[a][:].bitcast(U32), "p m t")
-        v_codes[1, 1] = shared.tile([P, HALF], U32, name="v_codes1_1", offset=4 * HALF * PACK, align_bytes=64)
+        v_codes[1, 1] = shared.tile([P, HALF], U32, name="v_codes1_1", offset=4 * HALF * PACK, align_bytes=256)
         gather_codes(1, HALF, HALF)
 
         def stationary(kind, a, t):
@@ -355,13 +355,13 @@ def tile_list_fresh_passage_banks_kernel(
         early0 = sb("wa_early0", [P, 2 * H], BF16)
         nc.vector.tensor_copy(*wa_views(early0[:], 0, 0, "p m k t"))
         quantise_wa(0, 0, 1, early0[:])
-        early1 = shared.tile([P, 2 * H], BF16, name="wa_early1", offset=BC_AT + 2 * HALF, align_bytes=64)
+        early1 = shared.tile([P, 2 * H], BF16, name="wa_early1", offset=BC_AT + 2 * HALF, align_bytes=256)
         nc.vector.tensor_copy(*wa_views(early1[:], 1, 0, "p m k t"))
         quantise_wa(0, 1, 1, early1[:])
         for s in (4, 5):
             make_c(s)
             max_bc(s)
-        late = shared.tile([P, PASSES, 2 * H], BF16, name="wa_late", offset=0, align_bytes=64)
+        late = shared.tile([P, PASSES, 2 * H], BF16, name="wa_late", offset=0, align_bytes=256)
         for a in range(PASSES):
             nc.scalar.copy(*wa_views(late[:, a, :], a, 1, "p m k t"))
         h_f32[0] = sb("h_first", [P, PACK, HALF], F32)

from contextlib import ExitStack

import concourse.mybir as mybir
from concourse.masks import make_identity

K, T, S, H, N = 1024, 2048, 1024, 512, 256
FLOPS = 2 * K * H * S * 3 + 2 * H * N * S

F32 = mybir.dt.float32
BF16 = mybir.dt.bfloat16
I32 = mybir.dt.int32
U32 = mybir.dt.uint32
U16 = mybir.dt.uint16
U8 = mybir.dt.uint8
E4M3 = mybir.dt.float8_e4m3fn_x4
E2M1 = mybir.dt.float4_e2m1fn_x4
MAX = mybir.AluOpType.max
MULT = mybir.AluOpType.mult
ADD = mybir.AluOpType.add
IDENTITY = mybir.ActivationFunctionType.Identity
COPY = mybir.ActivationFunctionType.Copy
RELU = mybir.ActivationFunctionType.Relu

P = 128
PACK = 4
PASSES = K // (P * PACK)
HALF = 512
UNITS = PACK * S // HALF
CHUNKS = ((0, 256), (256, 256), (512, 256), (768, 128), (896, 128))
BANKS = {"a": (2, 3, 6, 7, 2, 3), "b": (4, 5, 6, 7, 0, 1, 2, 1), "c": (0, 1, 2, 3, 4, 5, 1, 3)}
TURN_BANKS = ((4, 5), (0, 1))
C_AT = {2: 0, 3: 4 * HALF * (PACK - 1), 4: 4 * HALF * (PACK - 1)}
BC_AT = 4 * HALF * (PACK + 1)
QUARTER = HALF // 2
LIVE = 96
STAGE = 64


def tile_list_fresh_passage_banks_kernel(
    tc, tab_words, tab_scales, offs, wa, wb_words, wb_scales, wc_words, wc_scales, gT, w2, b2, out
):
    nc = tc.nc
    with ExitStack() as ctx:
        keep = ctx.enter_context(tc.tile_pool(name="keep", bufs=1))
        shared = ctx.enter_context(tc.tile_pool(name="shared", bufs=1))
        psum = ctx.enter_context(tc.psum_pool(name="psum", bufs=1))

        def sb(name, shape, dtype, tag=""):
            return keep.tile(shape, dtype, name=name, tag=tag or name, align_bytes=256)

        def bank(name, i):
            return psum.tile([P, HALF], F32, name=name, offset=2048 * i)

        offsets = keep.tile([P, S // 16], U16, name="offsets")
        nc.sync.dma_start(offsets[:], offs)

        def picks(j0, width):
            return offsets[:, j0 // 16 : (j0 + width) // 16]

        w_rows = sb("w_rows", [P, H], U8)
        for w, scales in enumerate((wc_scales, wb_scales)):
            nc.scalar.dma_start(
                w_rows[STAGE + w : P : 2, :].bitcast(I32), scales.rearrange("a q e -> q a e").bitcast(I32)
            )
        tab_plane = sb("tab_plane", [P, T], U8)
        nc.sync.dma_start(tab_plane[LIVE:P, :].bitcast(I32), tab_scales.rearrange("a q t -> q a t").bitcast(I32))
        nc.vector.memset(w_rows[0:STAGE, :].bitcast(I32), 0)
        nc.vector.memset(tab_plane[0:LIVE, :].bitcast(I32), 0)
        w_planes = sb("w_planes", [P, 2 * PASSES * H], U8)
        nc.vector.memset(w_planes[:].bitcast(I32), 0)
        v_planes = sb("v_planes", [P, PASSES * S], U8)
        nc.vector.memset(v_planes[:].bitcast(I32), 0)

        tab_w, wa_raw, fresh = {}, {}, {}

        def load_tab(a):
            tab_w[a] = sb("tab_w%d" % a, [P, T], I32)
            nc.sync.dma_start(tab_w[a][:], tab_words[a].rearrange("p t i -> p (t i)").bitcast(I32))

        def load_wa(a):
            wa_raw[a] = sb("wa_raw%d" % a, [P, PACK, H], F32)
            nc.sync.dma_start(wa_raw[a][:], wa[512 * a : 512 * (a + 1), :].rearrange("(p i) e -> p i e", i=PACK))

        def load_fresh(t):
            fresh[t] = sb("fresh%d" % t, [P, T], F32)
            nc.sync.dma_start(fresh[t][:], gT.rearrange("(p t) c -> t p c", t=PACK)[t])

        load_tab(0)
        wc_raw = sb("wc_raw", [P, PASSES, H // 2], I32)
        nc.sync.dma_start(wc_raw[:], wc_words.rearrange("a p e -> p a e").bitcast(I32))

        def deal(copy, dealt, raw, order):
            copy(dealt.rearrange("p (t m) -> " + order, t=PACK), raw.rearrange("p (m t) -> " + order, t=PACK))

        w_rows_dealt = sb("w_rows_dealt", [P, H], U8)
        deal(nc.vector.tensor_copy, w_rows_dealt[:], w_rows[:], "p t m")
        for q in (0, 2, 1, 3):
            nc.sync.dma_start(
                w_planes[32 * q : 32 * q + 4, :].bitcast(I32).rearrange("r (x e) -> r x e", x=2 * PASSES),
                w_rows_dealt[STAGE + 16 * q : STAGE + 16 * q + 16, :].bitcast(I32),
            )
        load_tab(1)
        picked_plane = sb("picked_plane", [P, S], U8)
        nc.vector.tensor_copy(picked_plane[:], tab_plane[:].indirect(offsets[:]))
        for q in (0, 2, 1, 3):
            nc.sync.dma_start(
                v_planes[32 * q : 32 * q + 4, :].bitcast(I32).rearrange("r (a j) -> r a j", a=PASSES),
                picked_plane[LIVE + 8 * q : LIVE + 8 * q + 8, :].bitcast(I32),
            )
        wb_raw = {}
        for a in range(PASSES):
            wb_raw[a] = shared.tile([P, H], I32, name="wb_raw%d" % a, offset=4 * HALF * (PACK - 1 + a))
            nc.sync.dma_start(wb_raw[a][:], wb_words[a].rearrange("p e i -> p (e i)").bitcast(I32))
        load_wa(0)
        load_wa(1)
        load_fresh(0)
        load_fresh(1)
        w2_raw = sb("w2_raw", [P, PACK, N], F32)
        nc.sync.dma_start(w2_raw[:], w2.rearrange("(p t) n -> p t n", t=PACK))
        load_fresh(2)
        load_fresh(3)
        bias = sb("bias", [P, N // P], F32)
        with nc.allow_non_contiguous_dma("one bias value for each partition"):
            nc.sync.dma_start(bias[:], b2.rearrange("(u p) -> p u", p=P))
        v_plane = [v_planes[:, a * S : (a + 1) * S] for a in range(PASSES)]

        v_codes = {(a, hf): sb("v_codes%d_%d" % (a, hf), [P, HALF], U32) for a, hf in ((0, 0), (0, 1), (1, 0))}

        def gather_codes(a, j0, width):
            hf, c0 = divmod(j0, HALF)
            nc.vector.tensor_copy(
                v_codes[a, hf][:, c0 : c0 + width], tab_w[a][:].bitcast(U32).indirect(picks(j0, width))
            )

        wa_codes = [sb("wa_codes%d" % pair, [P, PASSES, 2 * P], U32) for pair in range(2)]
        wa_plane = [sb("wa_plane%d" % pair, [P, PASSES, 2 * P], U8) for pair in range(2)]

        def wa_views(rounded, a, pair, order):
            raw = wa_raw[a][:].rearrange("p k (m u t) -> p u k m t", u=2, t=2)[:, pair]
            return rounded.rearrange("p (t m k) -> " + order, t=2, k=PACK), raw.rearrange("p k m t -> " + order)

        def quantise_wa(pair, a0, count, rounded):
            def flat(tile):
                return tile[:, a0 : a0 + count, :].rearrange("p a c -> p (a c)")

            nc.vector.quantize_mx(out=flat(wa_codes[pair]).bitcast(E4M3), scales=flat(wa_plane[pair]), in_=rounded)

        wc_codes = [sb("wc_codes%d" % a, [P, H], U16) for a in range(PASSES)]
        wb_codes = [sb("wb_codes%d" % a, [P, H], U32) for a in range(PASSES)]
        for a in range(PASSES):
            deal(nc.scalar.copy, wc_codes[a][:], wc_raw[:, a, :].bitcast(U16), "p t m")
        gather_codes(0, 0, HALF)
        gather_codes(0, HALF, HALF)
        gather_codes(1, 0, HALF)
        for a, copy in enumerate((nc.scalar.copy, nc.vector.tensor_copy)):
            deal(copy, wb_codes[a][:], wb_raw[a][:].bitcast(U32), "p m t")
        v_codes[1, 1] = shared.tile([P, HALF], U32, name="v_codes1_1", offset=4 * HALF * PACK, align_bytes=256)
        gather_codes(1, HALF, HALF)

        def stationary(kind, a, t):
            cols = slice(t * P, (t + 1) * P)
            if kind == "a":
                cols = slice(t % 2 * P, (t % 2 + 1) * P)
                return wa_codes[t // 2][:, a, cols].bitcast(E4M3), wa_plane[t // 2][:, a, cols]
            w = 1 if kind == "b" else 0
            e0 = (2 * a + w) * H + t * P
            if kind == "b":
                return wb_codes[a][:, cols].bitcast(E4M3), w_planes[:, e0 : e0 + P]
            return wc_codes[a][:, cols].bitcast(E2M1), w_planes[:, e0 : e0 + P]

        acc = {}

        def first_pass(kind, s, a):
            hf, t = divmod(s, PACK)
            if a == 0:
                acc[kind, s] = bank("acc_%s%d" % (kind, s), BANKS[kind][s])
            codes, scales = stationary(kind, a, t)
            moving_scales = v_plane[a][:, hf * HALF : (hf + 1) * HALF]
            nc.tensor.matmul_mx(
                out=acc[kind, s][:], lhsT=codes, lhsT_scale=scales,
                rhs=v_codes[a, hf][:].bitcast(E4M3), rhs_scale=moving_scales,
                start=(a == 0), stop=(a == PASSES - 1),
            )

        best_bc, best = {}, {}

        c_sb = {}

        def copy_c(s):
            if s in C_AT:
                c_sb[s] = shared.tile([P, HALF], F32, name="c_sb%d" % s, offset=C_AT[s])[:]
            else:
                c_sb[s] = sb("c_sb%d" % s, [P, HALF], F32)[:]
            nc.scalar.copy(c_sb[s], acc["c", s][:])

        def make_c(s):
            for a in range(PASSES):
                first_pass("c", s, a)
            copy_c(s)

        def max_bc(s):
            for a in range(PASSES):
                first_pass("b", s, a)
            if s < PACK:
                best_bc[s] = sb("best_bc%d" % s, [P, HALF], F32)[:]
            else:
                at = BC_AT + 4 * HALF * (s - PACK)
                best_bc[s] = shared.tile([P, HALF], F32, name="best_bc%d" % s, offset=at)[:]
            nc.vector.tensor_tensor(best_bc[s], acc["b", s][:], c_sb[s], MAX)

        def max_abc(s):
            if ("a", s) not in acc:
                for a in range(PASSES):
                    first_pass("a", s, a)
            width = CHUNKS[0][1] if s == PACK - 1 else HALF
            for c0 in range(0, HALF, width):
                if s == PACK:
                    best[s, c0] = shared.tile([P, HALF], F32, name="best4", offset=0)[:]
                else:
                    best[s, c0] = sb("best%d_%d" % (s, c0), [P, width], F32, "best3_0" if s == PACK + 1 else "")[:]
                cols = slice(c0, c0 + width)
                nc.vector.tensor_tensor(best[s, c0], acc["a", s][:, cols], best_bc[s][:, cols], MAX)

        identity = sb("identity", [P, P], F32)
        make_identity(nc, identity[:])

        def turn(dst, sources):
            for j in range(HALF // P):
                for i, src in enumerate(sources):
                    nc.tensor.matmul(
                        dst[:, j * P : (j + 1) * P], src(j), identity[:],
                        start=(i == 0), stop=(i == len(sources) - 1), is_transpose=True,
                    )

        def block_of(tiles, part):
            def block(j):
                i, c0 = divmod(j * P, QUARTER)
                return tiles[6 + i][:, part * QUARTER + c0 : part * QUARTER + c0 + P]

            return block

        def copy_out_bc(s):
            for a in range(PASSES):
                first_pass("c", s, a)
            minus_c[s] = sb("minus_c%d" % s, [P, HALF], F32)
            nc.scalar.activation(minus_c[s][:], acc["c", s][:], COPY, scale=-1.0)
            for a in range(PASSES):
                first_pass("b", s, a)
            b_sb[s] = sb("b_sb%d" % s, [P, HALF], F32)
            nc.scalar.copy(b_sb[s][:], acc["b", s][:])

        def lead_of_b(part):
            gap = bank("gap%d" % part, TURN_BANKS[part][0])
            turn(gap, (block_of(b_sb, part), block_of(minus_c, part)))
            minus_ct = bank("minus_ct%d" % part, TURN_BANKS[part][1])
            turn(minus_ct, (block_of(minus_c, part),))
            lead[part] = sb("lead%d" % part, [P, HALF], F32)
            nc.scalar.activation(lead[part][:], gap[:], RELU)
            c_t[part] = sb("c_t%d" % part, [P, HALF], F32)
            nc.scalar.activation(c_t[part][:], minus_ct[:], COPY, scale=-1.0)

        def turn_back(part):
            top_bc[part] = bank("top_bc%d" % part, TURN_BANKS[part][1])
            turn(top_bc[part], [lambda j, tile=tile: tile[:, j * P : (j + 1) * P] for tile in (lead[part], c_t[part])])

        def copy_out_a(part):
            late_a = bank("late_a%d" % part, TURN_BANKS[part][0])
            for i in range(2):
                for a in range(PASSES):
                    codes, scales = stationary("a", a, 2 + i)
                    j0 = HALF + part * QUARTER
                    nc.tensor.matmul_mx(
                        out=late_a[:, i * QUARTER : (i + 1) * QUARTER], lhsT=codes, lhsT_scale=scales,
                        rhs=v_codes[a, 1][:, part * QUARTER : (part + 1) * QUARTER].bitcast(E4M3),
                        rhs_scale=v_plane[a][:, j0 : j0 + QUARTER], start=(a == 0), stop=(a == PASSES - 1),
                    )
            a_sb[part] = sb("a_sb%d" % part, [P, HALF], F32)
            nc.scalar.copy(a_sb[part][:], late_a[:])

        def max_off(part):
            both = sb("best_late%d" % part, [P, HALF], F32)
            nc.vector.tensor_tensor(both[:], top_bc[part][:], a_sb[part][:], MAX)
            for i, s in enumerate((6, 7)):
                best[s, part * QUARTER] = both[:, i * QUARTER : (i + 1) * QUARTER]

        minus_c, b_sb, lead, c_t, top_bc, a_sb = {}, {}, {}, {}, {}, {}
        h_f32 = {}

        def h_chunk(j0, width):
            if j0 < HALF:
                return h_f32[0][:, :, j0 : j0 + width]
            return h_f32[j0][:]

        def weigh(t, j0, width):
            hf, c0 = divmod(j0, HALF)
            s = hf * PACK + t
            first = c0 // QUARTER * QUARTER if s in (3, 6, 7) else 0
            chosen = best[s, first][:, c0 - first : c0 - first + width]
            nc.vector.tensor_tensor(h_chunk(j0, width)[:, t, :], fresh[t][:].indirect(picks(j0, width)), chosen, MULT)

        def interleave(copy, dst, src):
            copy(
                dst.rearrange("p (c i t) -> p c t i", t=PACK, i=4),
                src.rearrange("p t (c i) -> p c t i", i=4),
            )

        h_bf = {}

        def round_h(j0, width, copy):
            h_bf[j0] = sb("h_bf%d" % j0, [P, width * PACK], BF16)
            interleave(copy, h_bf[j0][:], h_chunk(j0, width))

        mixed = {}

        def mix(j0, width, banks):
            h_codes = sb("h_codes%d" % j0, [P, width], U32)
            h_plane = sb("h_plane%d" % j0, [P, width], U8)
            nc.vector.quantize_mx(out=h_codes[:].bitcast(E4M3), scales=h_plane[:], in_=h_bf[j0][:])
            for u in range(N // P):
                mixed[j0, u] = bank("y%d_%d" % (j0, u), banks[u])
                cols = slice(u * P, (u + 1) * P)
                nc.tensor.matmul_mx(
                    out=mixed[j0, u][:, 0:width], lhsT=w2_codes[:, cols].bitcast(E4M3), lhsT_scale=w2_plane[:, cols],
                    rhs=h_codes[:].bitcast(E4M3), rhs_scale=h_plane[:], start=True, stop=True,
                )

        def finish(j0, width, last):
            res = sb("res%d" % j0, [P, N // P, width], F32)
            for u in range(N // P):
                y = mixed[j0, u][:, 0:width]
                if last and u == 1:
                    nc.vector.tensor_scalar_add(res[:, u, :], y, bias[:, u : u + 1])
                else:
                    nc.scalar.activation(res[:, u, :], y, IDENTITY, bias=bias[:, u : u + 1])
            nc.sync.dma_start(out[:, j0 : j0 + width].rearrange("(u p) j -> p u j", p=P), res[:])

        idle = bank("idle", BANKS["b"][PACK - 1])
        for i in range(3):
            nc.tensor.matmul_mx(
                out=idle[:], lhsT=tab_w[0][:, 0:P].bitcast(E4M3), lhsT_scale=tab_plane[:, 0:P],
                rhs=wc_raw[:, 0, :].bitcast(E2M1), rhs_scale=tab_plane[:, 0:HALF], start=True, stop=True,
            )
        for i in range(2):
            codes, scales = stationary("c", 0, 0)
            nc.tensor.matmul_mx(
                out=idle[:], lhsT=codes, lhsT_scale=scales,
                rhs=v_codes[0, 0][:].bitcast(E4M3), rhs_scale=w_planes[:, 0:HALF], start=True, stop=True,
            )
        for s in range(PACK):
            first_pass("c", s, 0)
        for s in range(PACK):
            first_pass("c", s, 1)
            copy_c(s)
            max_bc(s)
        early0 = sb("wa_early0", [P, 2 * H], BF16)
        nc.vector.tensor_copy(*wa_views(early0[:], 0, 0, "p m k t"))
        quantise_wa(0, 0, 1, early0[:])
        early1 = shared.tile([P, 2 * H], BF16, name="wa_early1", offset=BC_AT + 2 * HALF, align_bytes=256)
        nc.vector.tensor_copy(*wa_views(early1[:], 1, 0, "p m k t"))
        quantise_wa(0, 1, 1, early1[:])
        for s in (4, 5):
            make_c(s)
            max_bc(s)
        late = shared.tile([P, PASSES, 2 * H], BF16, name="wa_late", offset=0, align_bytes=256)
        for a in range(PASSES):
            nc.scalar.copy(*wa_views(late[:, a, :], a, 1, "p m k t"))
        h_f32[0] = sb("h_first", [P, PACK, HALF], F32)
        max_abc(0)
        max_abc(1)
        quantise_wa(1, 0, PASSES, late[:].rearrange("p a c -> p (a c)"))
        weigh(0, 0, HALF)
        weigh(1, 0, HALF)
        w2_bf = sb("w2_bf", [P, N * PACK], BF16, "best1_0")
        w2_codes = sb("w2_codes", [P, N], U32)
        w2_plane = sb("w2_plane", [P, N], U8)
        for s in (6, 7):
            copy_out_bc(s)
        max_abc(4)
        max_abc(2)
        max_abc(3)
        weigh(2, 0, HALF)
        for part in range(2):
            lead_of_b(part)
        copy_out_a(0)
        for a in range(PASSES):
            first_pass("a", 5, a)
        turn_back(0)
        copy_out_a(1)
        turn_back(1)
        nc.gpsimd.tensor_scalar(
            w2_bf[:].rearrange("p (n t) -> p n t", t=PACK), w2_raw[:].rearrange("p t n -> p n t"), 1.0, 0.0, MULT, ADD
        )
        nc.vector.quantize_mx(out=w2_codes[:].bitcast(E4M3), scales=w2_plane[:], in_=w2_bf[:])
        for j0, width in CHUNKS[:2]:
            weigh(PACK - 1, j0, width)
            round_h(j0, width, nc.scalar.copy)
        max_abc(5)
        h_tags = ("h_even", "h_odd", "h_even")
        for c in range(2, len(CHUNKS)):
            j0, width = CHUNKS[c]
            h_f32[j0] = sb("h_f32_%d" % j0, [P, PACK, width], F32, h_tags[c - 2])
            if c == 4:
                mix(*CHUNKS[2], (3, 0))
                finish(*CHUNKS[2], False)
            for t in range(PACK):
                if c == 2 and t == 2:
                    mix(*CHUNKS[0], (6, 7))
                    finish(*CHUNKS[0], False)
                if c in (2, 3) and t == 2:
                    max_off(c - 2)
                if c == 3 and t == 2:
                    mix(*CHUNKS[1], (2, 4))
                    finish(*CHUNKS[1], False)
                weigh(t, j0, width)
            if c < len(CHUNKS) - 1:
                round_h(j0, width, nc.scalar.copy)
        mix(*CHUNKS[3], (5, 1))
        finish(*CHUNKS[3], False)
        round_h(CHUNKS[-1][0], CHUNKS[-1][1], nc.vector.tensor_copy)
        mix(*CHUNKS[-1], (6, 7))
        finish(*CHUNKS[-1], True)
